import numpy as np
import ml_dtypes


def mxq(x, axis, fmt="e4m3"):
    dtype, down = {"e4m3": (ml_dtypes.float8_e4m3fn, 7), "e5m2": (ml_dtypes.float8_e5m2, 14)}[fmt]
    v = np.moveaxis(np.asarray(x, np.float32).astype(ml_dtypes.bfloat16).astype(np.float64), axis, -1)
    blocks = v.reshape(v.shape[:-1] + (-1, 32))
    amax = np.abs(blocks).max(-1, keepdims=True)
    byte = np.maximum(np.where(amax > 0, np.frexp(amax)[1] - 1 + 127, 0) - down, 1)
    scale = np.exp2(byte - 127.0)
    codes = (blocks / scale).astype(np.float32).astype(dtype).astype(np.float64)
    return np.moveaxis((codes * scale).reshape(v.shape), -1, axis)


WIDE = False


def mx_kscale(k):
    if not WIDE:
        return np.ones(k)
    levels = np.array([10, -10, 5, -5, 0])
    if k % 512:
        return np.exp2(np.random.permutation(np.resize(levels, k // 32))).repeat(32)
    a = np.empty((k // 512, 16))
    for p in range(k // 512):
        a[p, :8] = np.random.permutation(np.resize(levels, 8))
        for g in range(8):
            far = levels[np.abs(levels - a[p, g]) >= 10]
            a[p, g + 8] = far[np.random.randint(len(far))]
    return np.exp2(a.ravel()).repeat(32)


BF16 = ml_dtypes.bfloat16


def bf(x):
    return np.asarray(x, np.float32).astype(BF16)


def f64(x):
    return np.asarray(x).astype(np.float64)


E2M1 = np.array([0.0, 0.5, 1.0, 1.5, 2.0, 3.0, 4.0, 6.0, -0.0, -0.5, -1.0, -1.5, -2.0, -3.0, -4.0, -6.0])


def pack_weight(w, fmt):
    k, n = w.shape
    w = f64(bf(w)).reshape(k // 32, 32, n)
    amax = np.abs(w).max(1)
    if fmt == "e4m3":
        byte = np.frexp(amax)[1] - 1 + 127 - 7
    else:
        mant, ex = np.frexp(amax / 6.0)
        byte = np.where(mant > 0.5, ex, ex - 1) + 127
    byte = np.clip(np.where(amax > 0, byte, 1), 1, 254)
    scaled = (w * np.exp2(127.0 - byte)[:, None, :]).reshape(k, n).astype(np.float32)
    by_word = np.ascontiguousarray(scaled.reshape(k // 512, 128, 4, n).transpose(0, 1, 3, 2))
    if fmt == "e4m3":
        words = by_word.astype(ml_dtypes.float8_e4m3fn).view(np.uint8)
    else:
        c = by_word.astype(ml_dtypes.float4_e2m1fn).view(np.uint8) & 0xF
        words = c[..., 0::2] | (c[..., 1::2] << 4)
    return np.ascontiguousarray(words), np.ascontiguousarray(byte.astype(np.uint8).reshape(k // 512, 16, n))


def unpack_weight(words, scales, fmt):
    g, p, n, _ = words.shape
    if fmt == "e4m3":
        vals = np.ascontiguousarray(words).view(ml_dtypes.float8_e4m3fn).astype(np.float64)
    else:
        nib = np.empty((g, p, n, 4), np.uint8)
        nib[..., 0::2] = words & 0xF
        nib[..., 1::2] = words >> 4
        vals = E2M1[nib]
    vals = vals * np.repeat(np.exp2(scales.astype(np.float64) - 127.0), 8, axis=1)[..., None]
    return vals.transpose(0, 1, 3, 2).reshape(g * 512, n)
def pack4(w):
    words, scales = pack_weight(w, "e2m1")
    return words.reshape(words.shape[0], 128, -1), scales


def unpack4(words, scales):
    return unpack_weight(words.reshape(words.shape[0], 128, -1, 2), scales, "e2m1")


ZONES, L, NODES, C = 3, 512, 1536, 1024


def setup_inputs():
    s, t = mx_kscale(NODES), mx_kscale(C)
    x = np.random.standard_normal((NODES, C)) * s[:, None] * t
    up = 0.33 * np.random.standard_normal((NODES, NODES)) / np.sqrt(NODES) / s[:, None] * s
    mix = 0.5 * np.random.standard_normal((C, C)) / np.sqrt(C) / t[:, None] * t
    zone = np.random.standard_normal((NODES, L)) / np.sqrt(L) / s[:, None]
    valve = np.random.uniform(0.25, 1.0, (ZONES, C)) / t
    up_words, up_scales = pack4(up)
    mix_words, mix_scales = pack4(mix)
    zone_words, zone_scales = pack4(zone)
    return {"x": bf(x), "up_words": up_words, "up_scales": up_scales,
            "mix_words": mix_words, "mix_scales": mix_scales,
            "zone_words": zone_words, "zone_scales": zone_scales, "valve": bf(valve)}


def reference(x, up_words, up_scales, mix_words, mix_scales, zone_words, zone_scales, valve):
    x = f64(x)
    up = unpack4(up_words, up_scales)
    mix = unpack4(mix_words, mix_scales)
    zone = unpack4(zone_words, zone_scales).reshape(ZONES, L, L)
    h1 = x + (up.T @ mxq(x, 0, "e4m3"))
    h2 = h1 + np.maximum(mxq(h1, 1, "e4m3") @ mix, 0.0)
    hz = mxq(h2.reshape(ZONES, L, C), 1, "e4m3")
    return f64(valve)[:, None, :] * (zone.swapaxes(1, 2) @ hz)

@@ -1,0 +1,556 @@
+from contextlib import ExitStack
+
+import concourse.mybir as mybir
+from concourse.masks import make_identity
+
+ZONES, L, NODES, C = 3, 512, 1536, 1024
+FLOPS = 2 * (NODES * NODES * C + NODES * C * C + NODES * L * C)
+F32 = mybir.dt.float32
+BF16 = mybir.dt.bfloat16
+U32 = mybir.dt.uint32
+I32 = mybir.dt.int32
+U8 = mybir.dt.uint8
+FP8X4 = mybir.dt.float8_e4m3fn_x4
+FP4X4 = mybir.dt.float4_e2m1fn_x4
+P = 128
+ALU = mybir.AluOpType
+
+def tile_water_zone_transfer_t2_kernel(
+    tc, x, up_words, up_scales, mix_words, mix_scales, zone_words, zone_scales, valve, out
+):
+    nc = tc.nc
+    with ExitStack() as ctx:
+        keep = ctx.enter_context(tc.tile_pool(name="keep", bufs=1))
+        work = ctx.enter_context(tc.tile_pool(name="work", bufs=3))
+        psum = ctx.enter_context(tc.psum_pool(name="psum", bufs=1))
+        ctx.enter_context(tc.manual_schedule())
+
+        u_raw = [keep.tile([P, 3, 1024], U8, name="u_raw%d" % z, align_bytes=64) for z in range(3)]
+        u_perm = [keep.tile([P, 3, 1024], U8, name="u_perm%d" % z, align_bytes=64) for z in range(3)]
+        us_raw = keep.tile([P, 3, 1536], U8, name="us_raw", align_bytes=64)
+        us_perm = [keep.tile([P, 3, 512], U8, name="us_perm%d" % z, align_bytes=64) for z in range(3)]
+        mix_w = keep.tile([P, 2, 2048], U8, name="mix_w", align_bytes=64)
+        mix_s = keep.tile([P, 2, 1024], U8, name="mix_s", align_bytes=64)
+        zone_w = keep.tile([P, 3, 1024], U8, name="zone_w", align_bytes=64)
+        zone_s = keep.tile([P, 3, 512], U8, name="zone_s", align_bytes=64)
+        valve_b = keep.tile([P, 3072], BF16, name="valve_b", align_bytes=64)
+        ident = keep.tile([P, P], F32, name="ident", align_bytes=64)
+        warm = keep.tile([P, 2], F32, name="warm", align_bytes=64)
+        xr = [[keep.tile([P, 4, 512], BF16, name="xr%d%d" % (g, h), align_bytes=64) for h in range(2)] for g in range(3)]
+        xq = [[keep.tile([P, 512], U32, name="xq%d%d" % (g, h), align_bytes=64) for h in range(2)] for g in range(3)]
+        xs = [[keep.tile([P, 512], U8, name="xs%d%d" % (g, h), align_bytes=64) for h in range(2)] for g in range(3)]
+        h1 = [keep.tile([P, 4, 1024], F32, name="h1_%d" % z, align_bytes=64) for z in range(3)]
+        xi, h1b, h1t, h1q, h1s, h2, h2q, h2s, banks = {}, {}, {}, {}, {}, {}, {}, {}, {}
+
+        nc.vector.memset(us_raw[:].rearrange("p g n -> p (g n)").bitcast(I32), 0)
+        nc.gpsimd.memset(warm[:], 0.0)
+        nc.gpsimd.memset(mix_s[:].rearrange("p g n -> p (g n)").bitcast(I32), 0)
+        nc.gpsimd.memset(zone_s[:].rearrange("p g n -> p (g n)").bitcast(I32), 0)
+        make_identity(nc, ident[:])
+        nc.scalar.copy(out=warm[:, 1:2], in_=warm[:, 0:1])
+
+        up_v = up_words.rearrange("g p n -> p g n")
+        x_v = x.rearrange("(g p j) c -> g p j c", p=P, j=4)
+
+        def load_u(z):
+            nc.sync.dma_start(out=u_raw[z][:].bitcast(I32), in_=up_v[:, :, z * 1024 : (z + 1) * 1024].bitcast(I32))
+
+        def load_scales(tile, src):
+            src_v = src.rearrange("g (q r) n -> r q g n", r=4)
+            for r in range(4):
+                nc.sync.dma_start(out=tile[r:P:32, :, :].bitcast(I32), in_=src_v[r].bitcast(I32))
+
+        def load_x(g, h):
+            nc.sync.dma_start(out=xr[g][h][:], in_=x_v[g][:, :, h * 512 : (h + 1) * 512])
+
+        for g in range(3):
+            nc.sync.dma_start(out=u_raw[0][:, g, :].bitcast(I32), in_=up_v[:, g, 0:1024].bitcast(I32))
+            load_x(g, 0)
+            if g == 0:
+                load_scales(us_raw, up_scales)
+        load_u(1)
+        for g in range(3):
+            load_x(g, 1)
+        load_u(2)
+        load_scales(mix_s, mix_scales)
+        nc.sync.dma_start(out=mix_w[:].bitcast(I32), in_=mix_words.rearrange("g p n -> p g n").bitcast(I32))
+        load_scales(zone_s, zone_scales)
+        nc.sync.dma_start(out=zone_w[:].bitcast(I32), in_=zone_words.rearrange("g p n -> p g n").bitcast(I32))
+        nc.sync.dma_start(out=valve_b[:], in_=valve.rearrange("z c -> (z c)").partition_broadcast(P))
+
+        def cU(z, g):
+            nc.vector.tensor_copy(
+                out=u_perm[z][:, g, :].rearrange("p (t m b) -> p t m b", t=4, b=2),
+                in_=u_raw[z][:, g, :].rearrange("p (m t b) -> p t m b", t=4, b=2),
+            )
+
+        def cS(z):
+            nc.vector.tensor_copy(
+                out=us_perm[z][:].rearrange("p g (t m) -> p g t m", t=4),
+                in_=us_raw[:, :, z * 512 : (z + 1) * 512].rearrange("p g (m t) -> p g t m", t=4),
+            )
+
+        def inter(eng, g, h, c0, c1):
+            if (g, h) not in xi:
+                t = work.tile([P, 512, 4], BF16, name="xi", align_bytes=64)
+                xi[g, h] = t
+            dst = xi[g, h][:, c0:c1, :].rearrange("p (c i) j -> p c j i", i=4)
+            src = xr[g][h][:, :, c0:c1].rearrange("p j (c i) -> p c j i", i=4)
+            if eng == "V":
+                nc.vector.tensor_copy(out=dst, in_=src)
+            else:
+                nc.scalar.copy(out=dst, in_=src)
+
+        def aV(g, h, fr):
+            inter("V", g, h, 0, fr)
+
+        def aS(g, h, fr):
+            inter("S", g, h, fr, 512)
+
+        def b(g, h):
+            nc.vector.quantize_mx(
+                out=xq[g][h][:].bitcast(FP8X4), scales=xs[g][h][:], in_=xi[g, h][:].rearrange("p c j -> p (c j)")
+            )
+
+        def bank(key, k):
+            t = psum.tile([P, 512], F32, name="bank", tag="bank", bufs=8)
+            banks[key] = t
+            return t
+
+        def S1p(z, t, h, g, k=0):
+            if g == 0:
+                bank(("1", z, t, h), k)
+            nc.tensor.matmul_mx(
+                out=banks["1", z, t, h][:],
+                lhsT=u_perm[z][:, g, t * 256 : (t + 1) * 256].bitcast(FP4X4),
+                lhsT_scale=us_perm[z][:, g, t * P : (t + 1) * P],
+                rhs=xq[g][h][:].bitcast(FP8X4),
+                rhs_scale=xs[g][h][:],
+                start=(g == 0),
+                stop=(g == 2),
+            )
+
+        dts, kts = {}, {}
+
+        def dd(z, t, h, mode):
+            dst = h1[z][:, t, h * 512 : (h + 1) * 512]
+            nc.vector.tensor_tensor(out=dst, in0=banks["1", z, t, h][:], in1=xr[z][h][:, t, :], op=ALU.add)
+
+        def ddS(z, t, h):
+            dt = work.tile([P, 512], F32, name="dt", bufs=3, align_bytes=64)
+            dts[z, t, h] = dt
+            nc.scalar.copy(out=dt[:], in_=banks["1", z, t, h][:])
+
+        def ddG(z, t, h):
+            dst = h1[z][:, t, h * 512 : (h + 1) * 512]
+            nc.gpsimd.tensor_tensor(out=dst, in0=dts[z, t, h][:], in1=xr[z][h][:, t, :], op=ALU.add)
+
+        def e(z, t, h, eng):
+            t_ = work.tile([P, 512], BF16, name="h1b", bufs=12, align_bytes=64)
+            h1b[z, t, h] = t_
+            copier = nc.scalar.copy if eng == "S" else nc.vector.tensor_copy
+            copier(
+                out=t_[:].rearrange("p (u q e) -> p u q e", u=2, e=2),
+                in_=h1[z][:, t, h * 512 : (h + 1) * 512].rearrange("p (q u e) -> p u q e", u=2, e=2),
+            )
+
+        def T(z, h, tp, k=0):
+            bk = bank(("t", z, h, tp), k)
+            for i in range(2):
+                words = h1b[z, 2 * tp + i, h][:].bitcast(F32)
+                for u in range(2):
+                    nc.tensor.transpose(
+                        bk[:, (2 * i + u) * P : (2 * i + u + 1) * P], words[:, u * P : (u + 1) * P], ident[:]
+                    )
+
+        def f(z, h, tp, eng):
+            t_ = work.tile([P, 1024], BF16, name="h1t", bufs=4, align_bytes=64)
+            h1t[z, h, tp] = t_
+            copier = nc.scalar.copy if eng == "S" else nc.vector.tensor_copy
+            copier(
+                out=t_[:].bitcast(F32).rearrange("p (i n u) -> p i n u", i=2, u=2),
+                in_=banks["t", z, h, tp][:].rearrange("p (i u n) -> p i n u", i=2, u=2),
+            )
+
+        def q1(z, h, tp):
+            tq = work.tile([P, 256], U32, name="h1q", bufs=12, align_bytes=64)
+            ts = work.tile([P, 256], U8, name="h1s", bufs=12, align_bytes=64)
+            h1q[z, h, tp], h1s[z, h, tp] = tq, ts
+            nc.vector.quantize_mx(out=tq[:].bitcast(FP8X4), scales=ts[:], in_=h1t[z, h, tp][:])
+
+        def S2(z, bb, k=0):
+            bk = bank(("2", z, bb), k)
+            for t in range(4):
+                cols = slice((t % 2) * P, (t % 2 + 1) * P)
+                for g in range(2):
+                    nc.tensor.matmul_mx(
+                        out=bk[:, t * P : (t + 1) * P],
+                        lhsT=h1q[z, g, t // 2][:, cols].bitcast(FP8X4),
+                        lhsT_scale=h1s[z, g, t // 2][:, cols],
+                        rhs=mix_w[:, g, bb * 256 : (bb + 1) * 256].bitcast(FP4X4),
+                        rhs_scale=mix_s[:, g, bb * P : (bb + 1) * P],
+                        start=(g == 0),
+                        stop=(g == 1),
+                    )
+
+        def hh(z, bb):
+            key = (z, bb // 4)
+            if key not in h2:
+                t_ = work.tile([P, 512, 4], BF16, name="h2", bufs=4, align_bytes=64)
+                tq = work.tile([P, 512], U32, name="h2q", bufs=4, align_bytes=64)
+                ts = work.tile([P, 512], U8, name="h2s", bufs=4, align_bytes=64)
+                h2[key], h2q[key], h2s[key] = t_, tq, ts
+            nc.vector.scalar_tensor_tensor(
+                out=h2[key][:, (bb % 4) * P : (bb % 4 + 1) * P, :],
+                in0=banks["2", z, bb][:].rearrange("p (t c) -> p c t", t=4),
+                scalar=0.0,
+                in1=h1[z][:, :, bb * P : (bb + 1) * P].rearrange("p t c -> p c t"),
+                op0=ALU.max,
+                op1=ALU.add,
+            )
+
+        def q2(z, bp):
+            key = (z, bp // 2)
+            cols = slice((bp % 2) * 256, (bp % 2 + 1) * 256)
+            nc.vector.quantize_mx(
+                out=h2q[key][:, cols].bitcast(FP8X4),
+                scales=h2s[key][:, cols],
+                in_=h2[key][:, cols, :].rearrange("p c t -> p (c t)"),
+            )
+
+        def S3(z, hf, m, k=0):
+            bk = bank(("3", z, hf, m), k)
+            nc.tensor.matmul_mx(
+                out=bk[:],
+                lhsT=zone_w[:, z, m * 256 : (m + 1) * 256].bitcast(FP4X4),
+                lhsT_scale=zone_s[:, z, m * P : (m + 1) * P],
+                rhs=h2q[z, hf][:].bitcast(FP8X4),
+                rhs_scale=h2s[z, hf][:],
+                start=True,
+                stop=True,
+            )
+
+        def kfin(z, hf, m, eng, src):
+            o = work.tile([P, 512], F32, name="o", bufs=6, align_bytes=64)
+            gate = valve_b[:, z * 1024 + hf * 512 : z * 1024 + (hf + 1) * 512]
+            eng.tensor_tensor(out=o[:], in0=src, in1=gate, op=ALU.mult)
+            nc.sync.dma_start(out=out[z, m * P : (m + 1) * P, hf * 512 : (hf + 1) * 512], in_=o[:])
+
+        def kk(z, hf, m, mode):
+            kfin(z, hf, m, nc.vector, banks["3", z, hf, m][:])
+
+        def kkS(z, hf, m):
+            kt = work.tile([P, 512], F32, name="kt", bufs=4, align_bytes=64)
+            kts[z, hf, m] = kt
+            nc.scalar.copy(out=kt[:], in_=banks["3", z, hf, m][:])
+
+        def kkG(z, hf, m):
+            kfin(z, hf, m, nc.gpsimd, kts[z, hf, m][:])
+
+        cU(0, 0)
+        aV(0, 0, 256)
+        aS(0, 0, 256)
+        cU(0, 1)
+        cS(1)
+        aS(1, 0, 256)
+        cU(0, 2)
+        aV(1, 0, 256)
+        aS(2, 0, 256)
+        cS(0)
+        cU(1, 0)
+        b(1, 0)
+        aS(0, 1, 0)
+        b(0, 0)
+        cU(1, 2)
+        S1p(0, 3, 0, 0)
+        aV(2, 0, 256)
+        S1p(0, 1, 0, 0)
+        S1p(0, 1, 0, 1)
+        cU(1, 1)
+        S1p(0, 2, 0, 0)
+        b(2, 0)
+        aS(1, 1, 0)
+        S1p(0, 2, 0, 1)
+        S1p(0, 0, 0, 0)
+        b(0, 1)
+        S1p(0, 1, 0, 2)
+        S1p(0, 2, 0, 2)
+        cU(2, 1)
+        S1p(0, 1, 1, 0)
+        S1p(0, 2, 1, 0)
+        cU(2, 0)
+        S1p(0, 3, 1, 0)
+        S1p(0, 0, 0, 1)
+        cU(2, 2)
+        S1p(0, 0, 1, 0)
+        aS(2, 1, 0)
+        S1p(0, 0, 0, 2)
+        b(1, 1)
+        S1p(0, 3, 0, 1)
+        S1p(0, 3, 0, 2)
+        cS(2)
+        S1p(0, 3, 1, 1)
+        S1p(0, 2, 1, 1)
+        S1p(0, 0, 1, 1)
+        dd(0, 3, 0, 'V')
+        S1p(0, 1, 1, 1)
+        dd(0, 0, 0, 'V')
+        e(0, 3, 0, 'S')
+        S1p(2, 3, 0, 0)
+        S1p(2, 3, 0, 1)
+        b(2, 1)
+        e(0, 0, 0, 'S')
+        S1p(2, 0, 1, 0)
+        S1p(2, 3, 0, 2)
+        dd(0, 2, 0, 'V')
+        S1p(0, 1, 1, 2)
+        S1p(0, 2, 1, 2)
+        dd(2, 3, 0, 'V')
+        e(0, 2, 0, 'S')
+        S1p(0, 3, 1, 2)
+        S1p(2, 1, 1, 0)
+        dd(0, 1, 1, 'V')
+        S1p(2, 1, 1, 1)
+        e(2, 3, 0, 'S')
+        S1p(2, 2, 1, 0)
+        dd(0, 3, 1, 'V')
+        S1p(2, 2, 1, 1)
+        e(0, 1, 1, 'S')
+        S1p(2, 2, 1, 2)
+        dd(0, 2, 1, 'V')
+        S1p(0, 0, 1, 2)
+        e(0, 3, 1, 'S')
+        S1p(2, 2, 0, 0)
+        S1p(2, 2, 0, 1)
+        dd(2, 2, 1, 'V')
+        e(0, 2, 1, 'S')
+        S1p(2, 2, 0, 2)
+        T(0, 0, 1)
+        dd(0, 0, 1, 'V')
+        e(2, 2, 1, 'S')
+        S1p(2, 1, 0, 0)
+        dd(2, 2, 0, 'V')
+        e(0, 0, 1, 'S')
+        S1p(2, 1, 0, 1)
+        S1p(2, 1, 0, 2)
+        dd(0, 1, 0, 'V')
+        f(0, 0, 1, 'S')
+        S1p(2, 3, 1, 0)
+        S1p(2, 3, 1, 1)
+        dd(2, 1, 0, 'V')
+        e(2, 2, 0, 'S')
+        S1p(2, 3, 1, 2)
+        S1p(2, 1, 1, 2)
+        q1(0, 0, 1)
+        e(0, 1, 0, 'S')
+        S1p(1, 1, 0, 0)
+        dd(2, 1, 1, 'V')
+        S1p(2, 0, 1, 1)
+        e(2, 1, 0, 'S')
+        S1p(2, 0, 1, 2)
+        dd(2, 3, 1, 'V')
+        S1p(2, 0, 0, 0)
+        e(2, 1, 1, 'S')
+        S1p(2, 0, 0, 1)
+        S1p(2, 0, 0, 2)
+        dd(2, 0, 1, 'V')
+        e(2, 3, 1, 'S')
+        T(0, 1, 0)
+        dd(2, 0, 0, 'V')
+        T(0, 0, 0)
+        e(2, 0, 1, 'S')
+        T(2, 1, 1)
+        e(2, 0, 0, 'S')
+        T(2, 1, 0)
+        T(0, 1, 1)
+        f(0, 0, 0, 'S')
+        T(2, 0, 0)
+        f(0, 1, 1, 'S')
+        T(2, 0, 1)
+        q1(0, 0, 0)
+        S1p(1, 0, 0, 0)
+        f(0, 1, 0, 'S')
+        q1(0, 1, 1)
+        S1p(1, 3, 1, 0)
+        S1p(1, 0, 0, 1)
+        f(2, 0, 1, 'S')
+        q1(0, 1, 0)
+        S1p(1, 3, 0, 0)
+        S1p(1, 3, 0, 1)
+        f(2, 1, 0, 'S')
+        q1(2, 0, 1)
+        S2(0, 7)
+        f(2, 0, 0, 'S')
+        q1(2, 1, 0)
+        S2(0, 0)
+        hh(0, 7)
+        f(2, 1, 1, 'S')
+        S2(0, 2)
+        q1(2, 0, 0)
+        hh(0, 0)
+        S2(0, 5)
+        hh(0, 2)
+        S2(0, 1)
+        hh(0, 5)
+        S2(0, 4)
+        hh(0, 1)
+        S2(0, 3)
+        hh(0, 4)
+        S2(0, 6)
+        hh(0, 3)
+        S1p(1, 0, 1, 0)
+        S1p(1, 0, 1, 1)
+        S1p(1, 2, 1, 0)
+        hh(0, 6)
+        S1p(1, 2, 1, 1)
+        S1p(1, 2, 0, 0)
+        q2(0, 1)
+        S1p(1, 2, 0, 1)
+        q2(0, 3)
+        S1p(1, 1, 1, 0)
+        q2(0, 2)
+        S1p(1, 1, 1, 1)
+        q2(0, 0)
+        S1p(1, 2, 0, 2)
+        S1p(1, 3, 0, 2)
+        q1(2, 1, 1)
+        S1p(1, 2, 1, 2)
+        dd(1, 3, 0, 'V')
+        S1p(1, 0, 0, 2)
+        S1p(1, 1, 1, 2)
+        dd(1, 2, 1, 'V')
+        S1p(1, 0, 1, 2)
+        e(1, 3, 0, 'S')
+        S2(2, 0)
+        dd(1, 0, 1, 'V')
+        e(1, 2, 1, 'S')
+        S2(2, 4)
+        dd(1, 1, 1, 'V')
+        e(1, 0, 1, 'S')
+        S3(0, 0, 1)
+        dd(1, 0, 0, 'V')
+        S1p(1, 1, 0, 1)
+        e(1, 1, 1, 'S')
+        S3(0, 0, 3)
+        dd(1, 2, 0, 'V')
+        S1p(1, 1, 0, 2)
+        e(1, 0, 0, 'S')
+        S2(2, 5)
+        dd(1, 1, 0, 'V')
+        e(1, 2, 0, 'S')
+        S3(0, 0, 0)
+        hh(2, 5)
+        S1p(1, 3, 1, 1)
+        e(1, 1, 0, 'S')
+        T(1, 0, 1)
+        hh(2, 0)
+        kkS(0, 0, 0)
+        T(1, 0, 0)
+        S1p(1, 3, 1, 2)
+        kkS(0, 0, 1)
+        hh(2, 4)
+        kkG(0, 0, 0)
+        S2(2, 3)
+        f(1, 0, 0, 'S')
+        dd(1, 3, 1, 'V')
+        S3(0, 0, 2)
+        kkS(0, 0, 3)
+        q2(2, 2)
+        S2(2, 7)
+        kkG(0, 0, 1)
+        q1(1, 0, 0)
+        kkS(0, 0, 2)
+        S2(2, 2)
+        hh(2, 3)
+        e(1, 3, 1, 'S')
+        T(1, 1, 0)
+        kkG(0, 0, 3)
+        hh(2, 7)
+        f(1, 0, 1, 'S')
+        T(1, 1, 1)
+        hh(2, 2)
+        S3(0, 1, 3)
+        f(1, 1, 0, 'S')
+        S2(2, 6)
+        kkG(0, 0, 2)
+        q1(1, 0, 1)
+        kkS(0, 1, 3)
+        q2(2, 1)
+        S3(0, 1, 0)
+        f(1, 1, 1, 'S')
+        q1(1, 1, 0)
+        S2(2, 1)
+        hh(2, 6)
+        kkG(0, 1, 3)
+        kkS(0, 1, 0)
+        S3(0, 1, 1)
+        q1(1, 1, 1)
+        S3(0, 1, 2)
+        kkS(0, 1, 1)
+        hh(2, 1)
+        S2(1, 1)
+        kkG(0, 1, 0)
+        kkS(0, 1, 2)
+        q2(2, 3)
+        S2(1, 2)
+        hh(1, 1)
+        S2(1, 0)
+        kkG(0, 1, 2)
+        q2(2, 0)
+        hh(1, 2)
+        S2(1, 3)
+        hh(1, 0)
+        S3(2, 0, 3)
+        kkG(0, 1, 1)
+        S3(2, 0, 1)
+        kkS(2, 0, 3)
+        S3(2, 1, 0)
+        hh(1, 3)
+        S2(1, 6)
+        kkS(2, 0, 1)
+        q2(1, 0)
+        kkG(2, 0, 3)
+        S3(2, 0, 0)
+        q2(1, 1)
+        S3(2, 1, 1)
+        hh(1, 6)
+        S3(1, 0, 3)
+        S3(1, 0, 1)
+        kk(2, 1, 0, 'V')
+        kkS(1, 0, 3)
+        S3(1, 0, 0)
+        kkG(2, 0, 1)
+        S2(1, 4)
+        kkS(1, 0, 0)
+        kk(2, 0, 0, 'V')
+        S2(1, 5)
+        kkS(1, 0, 1)
+        hh(1, 4)
+        kkG(1, 0, 3)
+        S3(2, 1, 2)
+        hh(1, 5)
+        S3(2, 0, 2)
+        S3(2, 1, 3)
+        S2(1, 7)
+        kk(2, 0, 2, 'V')
+        kkG(1, 0, 1)
+        kk(2, 1, 3, 'V')
+        S3(1, 0, 2)
+        kkS(1, 0, 2)
+        hh(1, 7)
+        kkG(1, 0, 0)
+        kk(2, 1, 2, 'V')
+        q2(1, 3)
+        kkG(1, 0, 2)
+        q2(1, 2)
+        kk(2, 1, 1, 'V')
+        S3(1, 1, 1)
+        S3(1, 1, 2)
+        kkS(1, 1, 1)
+        S3(1, 1, 0)
+        kk(1, 1, 2, 'V')
+        S3(1, 1, 3)
+        kkG(1, 1, 1)
+        kkS(1, 1, 3)
+        kk(1, 1, 0, 'V')
+        kkG(1, 1, 3)

@@ -25,25 +25,28 @@ def tile_water_zone_transfer_t2_kernel(
         psum = ctx.enter_context(tc.psum_pool(name="psum", bufs=1))
         ctx.enter_context(tc.manual_schedule())
 
-        u_raw = [keep.tile([P, 3, 1024], U8, name="u_raw%d" % z, align_bytes=64) for z in range(3)]
-        u_perm = [keep.tile([P, 3, 1024], U8, name="u_perm%d" % z, align_bytes=64) for z in range(3)]
-        us_raw = keep.tile([P, 3, 1536], U8, name="us_raw", align_bytes=64)
-        us_perm = [keep.tile([P, 3, 512], U8, name="us_perm%d" % z, align_bytes=64) for z in range(3)]
+        u_w = [keep.tile([P, 3, 1024], U8, name="u_w%d" % z, align_bytes=64) for z in range(3)]
+        u_s = keep.tile([P, 3, 1536], U8, name="u_s", align_bytes=64)
         mix_w = keep.tile([P, 2, 2048], U8, name="mix_w", align_bytes=64)
         mix_s = keep.tile([P, 2, 1024], U8, name="mix_s", align_bytes=64)
+        mixp_w = keep.tile([P, 2, 2048], U8, name="mixp_w", align_bytes=64)
+        mixp_s = keep.tile([P, 2, 1024], U8, name="mixp_s", align_bytes=64)
         zone_w = keep.tile([P, 3, 1024], U8, name="zone_w", align_bytes=64)
         zone_s = keep.tile([P, 3, 512], U8, name="zone_s", align_bytes=64)
         valve_b = keep.tile([P, 3072], BF16, name="valve_b", align_bytes=64)
         ident = keep.tile([P, P], F32, name="ident", align_bytes=64)
+        ident_b = keep.tile([P, P], BF16, name="ident_b", align_bytes=64)
         warm = keep.tile([P, 2], F32, name="warm", align_bytes=64)
         xr = [[keep.tile([P, 4, 512], BF16, name="xr%d%d" % (g, h), align_bytes=64) for h in range(2)] for g in range(3)]
         xq = [[keep.tile([P, 512], U32, name="xq%d%d" % (g, h), align_bytes=64) for h in range(2)] for g in range(3)]
         xs = [[keep.tile([P, 512], U8, name="xs%d%d" % (g, h), align_bytes=64) for h in range(2)] for g in range(3)]
-        h1 = [keep.tile([P, 4, 1024], F32, name="h1_%d" % z, align_bytes=64) for z in range(3)]
-        xi, h1b, h1t, h1q, h1s, h2, h2q, h2s, banks = {}, {}, {}, {}, {}, {}, {}, {}, {}
+        xt = [keep.tile([P, 8, 512], BF16, name="xt%d" % z, align_bytes=64) for z in range(3)]
+        h1 = [keep.tile([P, 8, 512], F32, name="h1_%d" % z, align_bytes=64) for z in range(3)]
+        xi, h1b, h1q, h1s, h2t, h2i, h2q, h2s, banks, dts, kts = {}, {}, {}, {}, {}, {}, {}, {}, {}, {}, {}
 
-        nc.vector.memset(us_raw[:].rearrange("p g n -> p (g n)").bitcast(I32), 0)
+        nc.vector.memset(u_s[:].rearrange("p g n -> p (g n)").bitcast(I32), 0)
         nc.gpsimd.memset(warm[:], 0.0)
+        make_identity(nc, ident_b[:])
         nc.gpsimd.memset(mix_s[:].rearrange("p g n -> p (g n)").bitcast(I32), 0)
         nc.gpsimd.memset(zone_s[:].rearrange("p g n -> p (g n)").bitcast(I32), 0)
         make_identity(nc, ident[:])
@@ -53,7 +56,7 @@ def tile_water_zone_transfer_t2_kernel(
         x_v = x.rearrange("(g p j) c -> g p j c", p=P, j=4)
 
         def load_u(z):
-            nc.sync.dma_start(out=u_raw[z][:].bitcast(I32), in_=up_v[:, :, z * 1024 : (z + 1) * 1024].bitcast(I32))
+            nc.sync.dma_start(out=u_w[z][:].bitcast(I32), in_=up_v[:, :, z * 1024 : (z + 1) * 1024].bitcast(I32))
 
         def load_scales(tile, src):
             src_v = src.rearrange("g (q r) n -> r q g n", r=4)
@@ -63,163 +66,177 @@ def tile_water_zone_transfer_t2_kernel(
         def load_x(g, h):
             nc.sync.dma_start(out=xr[g][h][:], in_=x_v[g][:, :, h * 512 : (h + 1) * 512])
 
-        for g in range(3):
-            nc.sync.dma_start(out=u_raw[0][:, g, :].bitcast(I32), in_=up_v[:, g, 0:1024].bitcast(I32))
-            load_x(g, 0)
-            if g == 0:
-                load_scales(us_raw, up_scales)
-        load_u(1)
+        def load_mix():
+            nc.sync.dma_start(out=mix_w[:].bitcast(I32), in_=mix_words.rearrange("g p n -> p g n").bitcast(I32))
+
+        def load_zone():
+            nc.sync.dma_start(out=zone_w[:].bitcast(I32), in_=zone_words.rearrange("g p n -> p g n").bitcast(I32))
+
+        def load_valve():
+            nc.sync.dma_start(out=valve_b[:], in_=valve.rearrange("z c -> (z c)").partition_broadcast(P))
+
+
+        load_x(0, 0)
+        load_x(1, 0)
+        load_u(0)
+        load_x(2, 0)
+        load_scales(u_s, up_scales)
         for g in range(3):
             load_x(g, 1)
-        load_u(2)
+        load_u(1)
         load_scales(mix_s, mix_scales)
-        nc.sync.dma_start(out=mix_w[:].bitcast(I32), in_=mix_words.rearrange("g p n -> p g n").bitcast(I32))
+        load_mix()
+        load_u(2)
         load_scales(zone_s, zone_scales)
-        nc.sync.dma_start(out=zone_w[:].bitcast(I32), in_=zone_words.rearrange("g p n -> p g n").bitcast(I32))
-        nc.sync.dma_start(out=valve_b[:], in_=valve.rearrange("z c -> (z c)").partition_broadcast(P))
+        load_zone()
+        load_valve()
 
-        def cU(z, g):
+
+        def cM(g, gc):
+            cols = slice(gc * 1024, (gc + 1) * 1024)
             nc.vector.tensor_copy(
-                out=u_perm[z][:, g, :].rearrange("p (t m b) -> p t m b", t=4, b=2),
-                in_=u_raw[z][:, g, :].rearrange("p (m t b) -> p t m b", t=4, b=2),
+                out=mixp_w[:, g, cols].rearrange("p (t q b) -> p t q b", t=4, b=2),
+                in_=mix_w[:, g, cols].rearrange("p (q t b) -> p t q b", t=4, b=2),
             )
 
-        def cS(z):
+        def cN():
             nc.vector.tensor_copy(
-                out=us_perm[z][:].rearrange("p g (t m) -> p g t m", t=4),
-                in_=us_raw[:, :, z * 512 : (z + 1) * 512].rearrange("p g (m t) -> p g t m", t=4),
+                out=mixp_s[:].rearrange("p g (h t q) -> p (g h) t q", h=2, t=4),
+                in_=mix_s[:].rearrange("p g (h q t) -> p (g h) t q", h=2, t=4),
             )
 
-        def inter(eng, g, h, c0, c1):
+        def inter(copy, g, h, t0, t1):
             if (g, h) not in xi:
-                t = work.tile([P, 512, 4], BF16, name="xi", align_bytes=64)
+                t = work.tile([P, 4, P, 4], BF16, name="xi", bufs=3, align_bytes=64)
                 xi[g, h] = t
-            dst = xi[g, h][:, c0:c1, :].rearrange("p (c i) j -> p c j i", i=4)
-            src = xr[g][h][:, :, c0:c1].rearrange("p j (c i) -> p c j i", i=4)
-            if eng == "V":
-                nc.vector.tensor_copy(out=dst, in_=src)
-            else:
-                nc.scalar.copy(out=dst, in_=src)
+            copy(
+                out=xi[g, h][:, t0:t1, :, :],
+                in_=xr[g][h][:].rearrange("p j (q t) -> p t q j", t=4)[:, t0:t1, :, :],
+            )
 
         def aV(g, h, fr):
-            inter("V", g, h, 0, fr)
+            inter(nc.vector.tensor_copy, g, h, 0, fr // P)
 
         def aS(g, h, fr):
-            inter("S", g, h, fr, 512)
+            inter(nc.scalar.copy, g, h, fr // P, 4)
 
         def b(g, h):
             nc.vector.quantize_mx(
-                out=xq[g][h][:].bitcast(FP8X4), scales=xs[g][h][:], in_=xi[g, h][:].rearrange("p c j -> p (c j)")
+                out=xq[g][h][:].bitcast(FP8X4), scales=xs[g][h][:], in_=xi[g, h][:].rearrange("p t q j -> p (t q j)")
             )
 
-        def bank(key, k):
-            t = psum.tile([P, 512], F32, name="bank", tag="bank", bufs=8)
+        def bank(key, dtype=F32):
+            t = psum.tile([P, 512], dtype, name="bank", tag="bank", bufs=8)
             banks[key] = t
             return t
 
-        def S1p(z, t, h, g, k=0):
+        def X(z, m):
+            bk = bank(("x", z, m), BF16)
+            src = xr[z][m // 4][:].rearrange("p j (q t) -> p j t q", t=4)
+            for j in range(4):
+                nc.tensor.transpose(bk[:, j * P : (j + 1) * P], src[:, j, m % 4, :], ident_b[:])
+
+        def y(z, m):
+            nc.scalar.copy(
+                out=xt[z][:, m, :].rearrange("p (q j) -> p q j", j=4),
+                in_=banks["x", z, m][:].rearrange("p (j q) -> p q j", j=4),
+            )
+
+        def S1p(z, m, g):
             if g == 0:
-                bank(("1", z, t, h), k)
+                bank(("1", z, m))
+            cols = slice((m % 4) * P, (m % 4 + 1) * P)
             nc.tensor.matmul_mx(
-                out=banks["1", z, t, h][:],
-                lhsT=u_perm[z][:, g, t * 256 : (t + 1) * 256].bitcast(FP4X4),
-                lhsT_scale=us_perm[z][:, g, t * P : (t + 1) * P],
-                rhs=xq[g][h][:].bitcast(FP8X4),
-                rhs_scale=xs[g][h][:],
+                out=banks["1", z, m][:],
+                lhsT=xq[g][m // 4][:, cols].bitcast(FP8X4),
+                lhsT_scale=xs[g][m // 4][:, cols],
+                rhs=u_w[z][:, g, :].bitcast(FP4X4),
+                rhs_scale=u_s[:, g, z * 512 : (z + 1) * 512],
                 start=(g == 0),
                 stop=(g == 2),
             )
 
-        dts, kts = {}, {}
+        def dd(z, m):
+            nc.vector.tensor_tensor(out=h1[z][:, m, :], in0=banks["1", z, m][:], in1=xt[z][:, m, :], op=ALU.add)
 
-        def dd(z, t, h, mode):
-            dst = h1[z][:, t, h * 512 : (h + 1) * 512]
-            nc.vector.tensor_tensor(out=dst, in0=banks["1", z, t, h][:], in1=xr[z][h][:, t, :], op=ALU.add)
-
-        def ddS(z, t, h):
+        def ddS(z, m):
             dt = work.tile([P, 512], F32, name="dt", bufs=3, align_bytes=64)
-            dts[z, t, h] = dt
-            nc.scalar.copy(out=dt[:], in_=banks["1", z, t, h][:])
+            dts[z, m] = dt
+            nc.scalar.copy(out=dt[:], in_=banks["1", z, m][:])
 
-        def ddG(z, t, h):
-            dst = h1[z][:, t, h * 512 : (h + 1) * 512]
-            nc.gpsimd.tensor_tensor(out=dst, in0=dts[z, t, h][:], in1=xr[z][h][:, t, :], op=ALU.add)
+        def ddG(z, m):
+            nc.gpsimd.tensor_tensor(out=h1[z][:, m, :], in0=dts[z, m][:], in1=xt[z][:, m, :], op=ALU.add)
 
-        def e(z, t, h, eng):
-            t_ = work.tile([P, 512], BF16, name="h1b", bufs=12, align_bytes=64)
-            h1b[z, t, h] = t_
-            copier = nc.scalar.copy if eng == "S" else nc.vector.tensor_copy
-            copier(
-                out=t_[:].rearrange("p (u q e) -> p u q e", u=2, e=2),
-                in_=h1[z][:, t, h * 512 : (h + 1) * 512].rearrange("p (q u e) -> p u q e", u=2, e=2),
+        def e(z, h, n):
+            if n == 0:
+                t_ = work.tile([P, 512, 4], BF16, name="h1b", bufs=2, align_bytes=64)
+                h1b[z, h] = t_
+            rows = slice(n * 256, (n + 1) * 256)
+            nc.scalar.copy(
+                out=h1b[z, h][:, rows, :].rearrange("p (n i) t -> p n t i", i=4),
+                in_=h1[z][:, 4 * h : 4 * h + 4, rows].rearrange("p t (n i) -> p n t i", i=4),
             )
 
-        def T(z, h, tp, k=0):
-            bk = bank(("t", z, h, tp), k)
-            for i in range(2):
-                words = h1b[z, 2 * tp + i, h][:].bitcast(F32)
-                for u in range(2):
-                    nc.tensor.transpose(
-                        bk[:, (2 * i + u) * P : (2 * i + u + 1) * P], words[:, u * P : (u + 1) * P], ident[:]
-                    )
-
-        def f(z, h, tp, eng):
-            t_ = work.tile([P, 1024], BF16, name="h1t", bufs=4, align_bytes=64)
-            h1t[z, h, tp] = t_
-            copier = nc.scalar.copy if eng == "S" else nc.vector.tensor_copy
-            copier(
-                out=t_[:].bitcast(F32).rearrange("p (i n u) -> p i n u", i=2, u=2),
-                in_=banks["t", z, h, tp][:].rearrange("p (i u n) -> p i n u", i=2, u=2),
-            )
-
-        def q1(z, h, tp):
-            tq = work.tile([P, 256], U32, name="h1q", bufs=12, align_bytes=64)
-            ts = work.tile([P, 256], U8, name="h1s", bufs=12, align_bytes=64)
-            h1q[z, h, tp], h1s[z, h, tp] = tq, ts
-            nc.vector.quantize_mx(out=tq[:].bitcast(FP8X4), scales=ts[:], in_=h1t[z, h, tp][:])
-
-        def S2(z, bb, k=0):
-            bk = bank(("2", z, bb), k)
-            for t in range(4):
-                cols = slice((t % 2) * P, (t % 2 + 1) * P)
-                for g in range(2):
-                    nc.tensor.matmul_mx(
-                        out=bk[:, t * P : (t + 1) * P],
-                        lhsT=h1q[z, g, t // 2][:, cols].bitcast(FP8X4),
-                        lhsT_scale=h1s[z, g, t // 2][:, cols],
-                        rhs=mix_w[:, g, bb * 256 : (bb + 1) * 256].bitcast(FP4X4),
-                        rhs_scale=mix_s[:, g, bb * P : (bb + 1) * P],
-                        start=(g == 0),
-                        stop=(g == 1),
-                    )
-
-        def hh(z, bb):
-            key = (z, bb // 4)
-            if key not in h2:
-                t_ = work.tile([P, 512, 4], BF16, name="h2", bufs=4, align_bytes=64)
-                tq = work.tile([P, 512], U32, name="h2q", bufs=4, align_bytes=64)
-                ts = work.tile([P, 512], U8, name="h2s", bufs=4, align_bytes=64)
-                h2[key], h2q[key], h2s[key] = t_, tq, ts
-            nc.vector.scalar_tensor_tensor(
-                out=h2[key][:, (bb % 4) * P : (bb % 4 + 1) * P, :],
-                in0=banks["2", z, bb][:].rearrange("p (t c) -> p c t", t=4),
-                scalar=0.0,
-                in1=h1[z][:, :, bb * P : (bb + 1) * P].rearrange("p t c -> p c t"),
-                op0=ALU.max,
-                op1=ALU.add,
-            )
-
-        def q2(z, bp):
-            key = (z, bp // 2)
-            cols = slice((bp % 2) * 256, (bp % 2 + 1) * 256)
+        def q1(z, h):
+            tq = work.tile([P, 512], U32, name="h1q", bufs=4, align_bytes=64)
+            ts = work.tile([P, 512], U8, name="h1s", bufs=4, align_bytes=64)
+            h1q[z, h], h1s[z, h] = tq, ts
             nc.vector.quantize_mx(
-                out=h2q[key][:, cols].bitcast(FP8X4),
-                scales=h2s[key][:, cols],
-                in_=h2[key][:, cols, :].rearrange("p c t -> p (c t)"),
+                out=tq[:].bitcast(FP8X4), scales=ts[:], in_=h1b[z, h][:].rearrange("p n t -> p (n t)")
             )
 
-        def S3(z, hf, m, k=0):
-            bk = bank(("3", z, hf, m), k)
+        def S2(z, m, g):
+            if g == 0:
+                bank(("2", z, m))
+            nc.tensor.matmul_mx(
+                out=banks["2", z, m][:],
+                lhsT=mixp_w[:, g, m * 256 : (m + 1) * 256].bitcast(FP4X4),
+                lhsT_scale=mixp_s[:, g, m * P : (m + 1) * P],
+                rhs=h1q[z, g][:].bitcast(FP8X4),
+                rhs_scale=h1s[z, g][:],
+                start=(g == 0),
+                stop=(g == 1),
+            )
+
+        def hh(z, m):
+            t_ = work.tile([P, 512], BF16, name="h2t", bufs=6, align_bytes=64)
+            h2t[z, m] = t_
+            acc = banks["2", z, m][:].rearrange("p (q u e) -> p u q e", u=2, e=2)
+            base = h1[z][:, m, :].rearrange("p (q u e) -> p u q e", u=2, e=2)
+            dst = t_[:].rearrange("p (u q e) -> p u q e", u=2, e=2)
+            for u in range(2):
+                nc.vector.scalar_tensor_tensor(
+                    out=dst[:, u, :, :], in0=acc[:, u, :, :], scalar=0.0, in1=base[:, u, :, :], op0=ALU.max, op1=ALU.add
+                )
+
+        def T(z, mp):
+            bk = bank(("t", z, mp))
+            for i in range(2):
+                words = h2t[z, 2 * mp + i][:].bitcast(F32).rearrange("p (u w) -> p u w", u=2)
+                for u in range(2):
+                    nc.tensor.transpose(bk[:, (2 * i + u) * P : (2 * i + u + 1) * P], words[:, u, :], ident[:])
+
+        def f(z, mp, eng):
+            if mp % 2 == 0:
+                t_ = work.tile([P, 512, 4], BF16, name="h2i", bufs=3, align_bytes=64)
+                h2i[z, mp // 2] = t_
+            dst = h2i[z, mp // 2][:, (mp % 2) * 256 : (mp % 2 + 1) * 256, :].rearrange("p c t -> p (c t)")
+            copy = nc.scalar.copy if eng == "S" else nc.vector.tensor_copy
+            copy(
+                out=dst.bitcast(F32).rearrange("p (i q u) -> p i q u", i=2, u=2),
+                in_=banks["t", z, mp][:].rearrange("p (i u q) -> p i q u", i=2, u=2),
+            )
+
+        def q2(z, hf):
+            tq = work.tile([P, 512], U32, name="h2q", bufs=3, align_bytes=64)
+            ts = work.tile([P, 512], U8, name="h2s", bufs=3, align_bytes=64)
+            h2q[z, hf], h2s[z, hf] = tq, ts
+            nc.vector.quantize_mx(
+                out=tq[:].bitcast(FP8X4), scales=ts[:], in_=h2i[z, hf][:].rearrange("p c t -> p (c t)")
+            )
+
+        def S3(z, hf, m):
+            bk = bank(("3", z, hf, m))
             nc.tensor.matmul_mx(
                 out=bk[:],
                 lhsT=zone_w[:, z, m * 256 : (m + 1) * 256].bitcast(FP4X4),
@@ -233,324 +250,360 @@ def tile_water_zone_transfer_t2_kernel(
         def kfin(z, hf, m, eng, src):
             o = work.tile([P, 512], F32, name="o", bufs=6, align_bytes=64)
             gate = valve_b[:, z * 1024 + hf * 512 : z * 1024 + (hf + 1) * 512]
-            eng.tensor_tensor(out=o[:], in0=src, in1=gate, op=ALU.mult)
+            eng.tensor_tensor(
+                out=o[:].rearrange("p (q t) -> p q t", t=4),
+                in0=src,
+                in1=gate.rearrange("p (q t) -> p q t", t=4),
+                op=ALU.mult,
+            )
             nc.sync.dma_start(out=out[z, m * P : (m + 1) * P, hf * 512 : (hf + 1) * 512], in_=o[:])
 
-        def kk(z, hf, m, mode):
-            kfin(z, hf, m, nc.vector, banks["3", z, hf, m][:])
+        def kk(z, hf, m):
+            kfin(z, hf, m, nc.vector, banks["3", z, hf, m][:].rearrange("p (t q) -> p q t", t=4))
 
         def kkS(z, hf, m):
             kt = work.tile([P, 512], F32, name="kt", bufs=4, align_bytes=64)
             kts[z, hf, m] = kt
-            nc.scalar.copy(out=kt[:], in_=banks["3", z, hf, m][:])
+            nc.scalar.copy(
+                out=kt[:].rearrange("p (q t) -> p q t", t=4),
+                in_=banks["3", z, hf, m][:].rearrange("p (t q) -> p q t", t=4),
+            )
 
         def kkG(z, hf, m):
-            kfin(z, hf, m, nc.gpsimd, kts[z, hf, m][:])
+            kfin(z, hf, m, nc.gpsimd, kts[z, hf, m][:].rearrange("p (q t) -> p q t", t=4))
 
-        cU(0, 0)
         aV(0, 0, 256)
         aS(0, 0, 256)
-        cU(0, 1)
-        cS(1)
-        aS(1, 0, 256)
-        cU(0, 2)
-        aV(1, 0, 256)
-        aS(2, 0, 256)
-        cS(0)
-        cU(1, 0)
-        b(1, 0)
-        aS(0, 1, 0)
+        X(0, 0)
+        X(0, 1)
+        y(0, 0)
         b(0, 0)
-        cU(1, 2)
-        S1p(0, 3, 0, 0)
+        X(1, 0)
+        aS(1, 0, 256)
+        X(0, 2)
+        aV(1, 0, 256)
+        X(1, 1)
+        X(1, 2)
+        y(0, 1)
+        b(1, 0)
+        X(1, 3)
+        y(0, 2)
+        X(0, 3)
         aV(2, 0, 256)
-        S1p(0, 1, 0, 0)
-        S1p(0, 1, 0, 1)
-        cU(1, 1)
-        S1p(0, 2, 0, 0)
+        X(2, 0)
+        y(1, 0)
+        S1p(0, 0, 0)
+        y(0, 3)
+        S1p(0, 1, 0)
+        y(1, 1)
+        S1p(0, 0, 1)
+        aS(2, 0, 256)
+        S1p(0, 2, 0)
+        S1p(0, 1, 1)
+        aV(0, 1, 256)
+        X(2, 1)
+        aS(0, 1, 256)
         b(2, 0)
-        aS(1, 1, 0)
-        S1p(0, 2, 0, 1)
-        S1p(0, 0, 0, 0)
+        S1p(0, 3, 0)
+        aV(1, 1, 256)
+        S1p(0, 2, 1)
+        y(1, 2)
+        S1p(0, 0, 2)
+        S1p(0, 3, 1)
+        aS(1, 1, 256)
         b(0, 1)
-        S1p(0, 1, 0, 2)
-        S1p(0, 2, 0, 2)
-        cU(2, 1)
-        S1p(0, 1, 1, 0)
-        S1p(0, 2, 1, 0)
-        cU(2, 0)
-        S1p(0, 3, 1, 0)
-        S1p(0, 0, 0, 1)
-        cU(2, 2)
-        S1p(0, 0, 1, 0)
-        aS(2, 1, 0)
-        S1p(0, 0, 0, 2)
+        S1p(0, 1, 2)
+        S1p(0, 2, 2)
+        dd(0, 0)
+        X(2, 2)
+        dd(0, 1)
+        S1p(0, 3, 2)
+        y(2, 0)
+        S1p(0, 4, 0)
         b(1, 1)
-        S1p(0, 3, 0, 1)
-        S1p(0, 3, 0, 2)
-        cS(2)
-        S1p(0, 3, 1, 1)
-        S1p(0, 2, 1, 1)
-        S1p(0, 0, 1, 1)
-        dd(0, 3, 0, 'V')
-        S1p(0, 1, 1, 1)
-        dd(0, 0, 0, 'V')
-        e(0, 3, 0, 'S')
-        S1p(2, 3, 0, 0)
-        S1p(2, 3, 0, 1)
+        y(1, 3)
+        S1p(0, 5, 0)
+        S1p(0, 6, 0)
+        dd(0, 2)
+        aS(2, 1, 256)
+        S1p(0, 4, 1)
+        S1p(0, 7, 0)
+        aV(2, 1, 256)
+        S1p(0, 5, 1)
+        S1p(0, 6, 1)
+        dd(0, 3)
+        S1p(0, 7, 1)
+        y(2, 1)
+        X(0, 4)
         b(2, 1)
-        e(0, 0, 0, 'S')
-        S1p(2, 0, 1, 0)
-        S1p(2, 3, 0, 2)
-        dd(0, 2, 0, 'V')
-        S1p(0, 1, 1, 2)
-        S1p(0, 2, 1, 2)
-        dd(2, 3, 0, 'V')
-        e(0, 2, 0, 'S')
-        S1p(0, 3, 1, 2)
-        S1p(2, 1, 1, 0)
-        dd(0, 1, 1, 'V')
-        S1p(2, 1, 1, 1)
-        e(2, 3, 0, 'S')
-        S1p(2, 2, 1, 0)
-        dd(0, 3, 1, 'V')
-        S1p(2, 2, 1, 1)
-        e(0, 1, 1, 'S')
-        S1p(2, 2, 1, 2)
-        dd(0, 2, 1, 'V')
-        S1p(0, 0, 1, 2)
-        e(0, 3, 1, 'S')
-        S1p(2, 2, 0, 0)
-        S1p(2, 2, 0, 1)
-        dd(2, 2, 1, 'V')
-        e(0, 2, 1, 'S')
-        S1p(2, 2, 0, 2)
-        T(0, 0, 1)
-        dd(0, 0, 1, 'V')
-        e(2, 2, 1, 'S')
-        S1p(2, 1, 0, 0)
-        dd(2, 2, 0, 'V')
-        e(0, 0, 1, 'S')
-        S1p(2, 1, 0, 1)
-        S1p(2, 1, 0, 2)
-        dd(0, 1, 0, 'V')
-        f(0, 0, 1, 'S')
-        S1p(2, 3, 1, 0)
-        S1p(2, 3, 1, 1)
-        dd(2, 1, 0, 'V')
-        e(2, 2, 0, 'S')
-        S1p(2, 3, 1, 2)
-        S1p(2, 1, 1, 2)
-        q1(0, 0, 1)
-        e(0, 1, 0, 'S')
-        S1p(1, 1, 0, 0)
-        dd(2, 1, 1, 'V')
-        S1p(2, 0, 1, 1)
-        e(2, 1, 0, 'S')
-        S1p(2, 0, 1, 2)
-        dd(2, 3, 1, 'V')
-        S1p(2, 0, 0, 0)
-        e(2, 1, 1, 'S')
-        S1p(2, 0, 0, 1)
-        S1p(2, 0, 0, 2)
-        dd(2, 0, 1, 'V')
-        e(2, 3, 1, 'S')
-        T(0, 1, 0)
-        dd(2, 0, 0, 'V')
-        T(0, 0, 0)
-        e(2, 0, 1, 'S')
-        T(2, 1, 1)
-        e(2, 0, 0, 'S')
-        T(2, 1, 0)
-        T(0, 1, 1)
-        f(0, 0, 0, 'S')
-        T(2, 0, 0)
-        f(0, 1, 1, 'S')
-        T(2, 0, 1)
-        q1(0, 0, 0)
-        S1p(1, 0, 0, 0)
-        f(0, 1, 0, 'S')
-        q1(0, 1, 1)
-        S1p(1, 3, 1, 0)
-        S1p(1, 0, 0, 1)
-        f(2, 0, 1, 'S')
-        q1(0, 1, 0)
-        S1p(1, 3, 0, 0)
-        S1p(1, 3, 0, 1)
-        f(2, 1, 0, 'S')
-        q1(2, 0, 1)
-        S2(0, 7)
-        f(2, 0, 0, 'S')
-        q1(2, 1, 0)
-        S2(0, 0)
-        hh(0, 7)
-        f(2, 1, 1, 'S')
-        S2(0, 2)
-        q1(2, 0, 0)
+        y(2, 2)
+        X(2, 3)
+        X(0, 5)
+        cN()
+        y(2, 3)
+        X(1, 4)
+        S1p(0, 4, 2)
+        y(0, 4)
+        S1p(0, 5, 2)
+        S1p(0, 6, 2)
+        cM(0, 0)
+        y(0, 5)
+        S1p(0, 7, 2)
+        X(0, 6)
+        dd(0, 4)
+        y(1, 4)
+        X(1, 5)
+        dd(0, 5)
+        y(0, 6)
+        X(2, 4)
+        X(0, 7)
+        y(1, 5)
+        X(2, 5)
+        dd(0, 6)
+        X(1, 6)
+        y(0, 7)
+        X(2, 6)
+        cM(0, 1)
+        X(2, 7)
+        y(1, 6)
+        X(1, 7)
+        dd(0, 7)
+        S1p(1, 0, 0)
+        e(0, 0, 0)
+        cM(1, 0)
+        S1p(1, 0, 1)
+        S1p(1, 0, 2)
+        cM(1, 1)
+        S1p(1, 1, 0)
+        S1p(1, 1, 1)
+        e(0, 0, 1)
+        dd(1, 0)
+        S1p(1, 1, 2)
+        S1p(1, 2, 0)
+        dd(1, 1)
+        S1p(1, 2, 1)
+        S1p(1, 2, 2)
+        S1p(1, 3, 0)
+        e(0, 1, 0)
+        q1(0, 0)
+        S1p(1, 3, 1)
+        S1p(1, 3, 2)
+        dd(1, 2)
+        S1p(1, 4, 0)
+        S1p(1, 4, 1)
+        dd(1, 3)
+        e(0, 1, 1)
+        S1p(1, 4, 2)
+        S1p(1, 5, 0)
+        dd(1, 4)
+        S1p(1, 5, 1)
+        S1p(1, 5, 2)
+        S1p(1, 6, 0)
+        y(1, 7)
+        dd(1, 5)
+        S1p(1, 6, 1)
+        S1p(1, 6, 2)
+        y(2, 4)
+        q1(0, 1)
+        S1p(1, 7, 0)
+        S1p(1, 7, 1)
+        e(1, 0, 0)
+        dd(1, 6)
+        S1p(1, 7, 2)
+        S2(0, 0, 0)
+        dd(1, 7)
+        S2(0, 0, 1)
+        S2(0, 1, 0)
+        e(1, 0, 1)
         hh(0, 0)
-        S2(0, 5)
-        hh(0, 2)
-        S2(0, 1)
-        hh(0, 5)
-        S2(0, 4)
+        S2(0, 1, 1)
+        S2(0, 2, 0)
         hh(0, 1)
-        S2(0, 3)
-        hh(0, 4)
-        S2(0, 6)
+        S2(0, 2, 1)
+        S2(0, 3, 0)
+        S2(0, 3, 1)
+        hh(0, 2)
+        e(1, 1, 0)
+        S2(0, 4, 0)
+        S2(0, 4, 1)
         hh(0, 3)
-        S1p(1, 0, 1, 0)
-        S1p(1, 0, 1, 1)
-        S1p(1, 2, 1, 0)
+        T(0, 0)
+        q1(1, 0)
+        e(1, 1, 1)
+        S2(0, 5, 0)
+        S2(0, 5, 1)
+        hh(0, 4)
+        S1p(2, 0, 0)
+        S1p(2, 0, 1)
+        hh(0, 5)
+        S1p(2, 0, 2)
+        y(2, 5)
+        S2(0, 6, 0)
+        dd(2, 0)
+        f(0, 0, 'S')
+        S2(0, 6, 1)
+        T(0, 1)
         hh(0, 6)
-        S1p(1, 2, 1, 1)
-        S1p(1, 2, 0, 0)
-        q2(0, 1)
-        S1p(1, 2, 0, 1)
-        q2(0, 3)
-        S1p(1, 1, 1, 0)
-        q2(0, 2)
-        S1p(1, 1, 1, 1)
+        y(2, 6)
+        S1p(2, 1, 0)
+        f(0, 1, 'S')
+        q1(1, 1)
+        S1p(2, 1, 1)
+        S1p(2, 1, 2)
+        S2(0, 7, 0)
         q2(0, 0)
-        S1p(1, 2, 0, 2)
-        S1p(1, 3, 0, 2)
-        q1(2, 1, 1)
-        S1p(1, 2, 1, 2)
-        dd(1, 3, 0, 'V')
-        S1p(1, 0, 0, 2)
-        S1p(1, 1, 1, 2)
-        dd(1, 2, 1, 'V')
-        S1p(1, 0, 1, 2)
-        e(1, 3, 0, 'S')
-        S2(2, 0)
-        dd(1, 0, 1, 'V')
-        e(1, 2, 1, 'S')
-        S2(2, 4)
-        dd(1, 1, 1, 'V')
-        e(1, 0, 1, 'S')
-        S3(0, 0, 1)
-        dd(1, 0, 0, 'V')
-        S1p(1, 1, 0, 1)
-        e(1, 1, 1, 'S')
-        S3(0, 0, 3)
-        dd(1, 2, 0, 'V')
-        S1p(1, 1, 0, 2)
-        e(1, 0, 0, 'S')
-        S2(2, 5)
-        dd(1, 1, 0, 'V')
-        e(1, 2, 0, 'S')
+        S2(0, 7, 1)
+        S1p(2, 2, 0)
+        hh(0, 7)
+        S1p(2, 2, 1)
+        S1p(2, 2, 2)
+        dd(2, 1)
         S3(0, 0, 0)
-        hh(2, 5)
-        S1p(1, 3, 1, 1)
-        e(1, 1, 0, 'S')
-        T(1, 0, 1)
-        hh(2, 0)
-        kkS(0, 0, 0)
-        T(1, 0, 0)
-        S1p(1, 3, 1, 2)
-        kkS(0, 0, 1)
-        hh(2, 4)
-        kkG(0, 0, 0)
-        S2(2, 3)
-        f(1, 0, 0, 'S')
-        dd(1, 3, 1, 'V')
-        S3(0, 0, 2)
-        kkS(0, 0, 3)
-        q2(2, 2)
-        S2(2, 7)
-        kkG(0, 0, 1)
-        q1(1, 0, 0)
-        kkS(0, 0, 2)
-        S2(2, 2)
-        hh(2, 3)
-        e(1, 3, 1, 'S')
-        T(1, 1, 0)
-        kkG(0, 0, 3)
-        hh(2, 7)
-        f(1, 0, 1, 'S')
-        T(1, 1, 1)
-        hh(2, 2)
-        S3(0, 1, 3)
-        f(1, 1, 0, 'S')
-        S2(2, 6)
-        kkG(0, 0, 2)
-        q1(1, 0, 1)
-        kkS(0, 1, 3)
-        q2(2, 1)
-        S3(0, 1, 0)
-        f(1, 1, 1, 'S')
-        q1(1, 1, 0)
-        S2(2, 1)
-        hh(2, 6)
-        kkG(0, 1, 3)
-        kkS(0, 1, 0)
-        S3(0, 1, 1)
-        q1(1, 1, 1)
-        S3(0, 1, 2)
-        kkS(0, 1, 1)
-        hh(2, 1)
-        S2(1, 1)
-        kkG(0, 1, 0)
-        kkS(0, 1, 2)
-        q2(2, 3)
-        S2(1, 2)
-        hh(1, 1)
-        S2(1, 0)
-        kkG(0, 1, 2)
-        q2(2, 0)
-        hh(1, 2)
-        S2(1, 3)
+        S2(1, 0, 0)
+        kk(0, 0, 0)
+        S2(1, 0, 1)
+        T(0, 2)
+        dd(2, 2)
+        S3(0, 0, 1)
+        f(0, 2, 'S')
         hh(1, 0)
-        S3(2, 0, 3)
-        kkG(0, 1, 1)
-        S3(2, 0, 1)
-        kkS(2, 0, 3)
-        S3(2, 1, 0)
+        S1p(2, 3, 0)
+        S1p(2, 3, 1)
+        y(2, 7)
+        kk(0, 0, 1)
+        S1p(2, 3, 2)
+        S2(1, 1, 0)
+        dd(2, 3)
+        S2(1, 1, 1)
+        S3(0, 0, 2)
+        hh(1, 1)
+        S1p(2, 4, 0)
+        S1p(2, 4, 1)
+        kk(0, 0, 2)
+        S1p(2, 4, 2)
+        S2(1, 2, 0)
+        dd(2, 4)
+        S2(1, 2, 1)
+        S3(0, 0, 3)
+        hh(1, 2)
+        T(0, 3)
+        T(1, 0)
+        kk(0, 0, 3)
+        f(0, 3, 'S')
+        S2(1, 3, 0)
+        S2(1, 3, 1)
+        f(1, 0, 'S')
+        q2(0, 1)
+        S1p(2, 5, 0)
+        S1p(2, 5, 1)
+        e(2, 0, 0)
         hh(1, 3)
-        S2(1, 6)
-        kkS(2, 0, 1)
-        q2(1, 0)
-        kkG(2, 0, 3)
-        S3(2, 0, 0)
-        q2(1, 1)
-        S3(2, 1, 1)
-        hh(1, 6)
-        S3(1, 0, 3)
-        S3(1, 0, 1)
-        kk(2, 1, 0, 'V')
-        kkS(1, 0, 3)
-        S3(1, 0, 0)
-        kkG(2, 0, 1)
-        S2(1, 4)
-        kkS(1, 0, 0)
-        kk(2, 0, 0, 'V')
-        S2(1, 5)
-        kkS(1, 0, 1)
+        S1p(2, 5, 2)
+        S3(0, 1, 0)
+        dd(2, 5)
+        S2(1, 4, 0)
+        S2(1, 4, 1)
+        e(2, 0, 1)
+        kk(0, 1, 0)
+        S1p(2, 6, 0)
+        S1p(2, 6, 1)
         hh(1, 4)
-        kkG(1, 0, 3)
-        S3(2, 1, 2)
+        S1p(2, 6, 2)
+        S3(0, 1, 1)
+        dd(2, 6)
+        S2(1, 5, 0)
+        S2(1, 5, 1)
+        kk(0, 1, 1)
+        S1p(2, 7, 0)
+        S1p(2, 7, 1)
         hh(1, 5)
-        S3(2, 0, 2)
-        S3(2, 1, 3)
-        S2(1, 7)
-        kk(2, 0, 2, 'V')
-        kkG(1, 0, 1)
-        kk(2, 1, 3, 'V')
-        S3(1, 0, 2)
-        kkS(1, 0, 2)
+        S1p(2, 7, 2)
+        T(1, 1)
+        q1(2, 0)
+        S2(1, 6, 0)
+        f(1, 1, 'S')
+        dd(2, 7)
+        S2(1, 6, 1)
+        S3(0, 1, 2)
+        hh(1, 6)
+        S2(1, 7, 0)
+        e(2, 1, 0)
+        S2(1, 7, 1)
+        kk(0, 1, 2)
+        S3(0, 1, 3)
+        T(1, 2)
         hh(1, 7)
-        kkG(1, 0, 0)
-        kk(2, 1, 2, 'V')
-        q2(1, 3)
-        kkG(1, 0, 2)
-        q2(1, 2)
-        kk(2, 1, 1, 'V')
-        S3(1, 1, 1)
-        S3(1, 1, 2)
-        kkS(1, 1, 1)
+        e(2, 1, 1)
+        q2(1, 0)
+        T(1, 3)
+        kk(0, 1, 3)
+        S3(1, 0, 0)
+        f(1, 2, 'S')
+        S3(1, 0, 1)
+        q1(2, 1)
+        S3(1, 0, 2)
+        f(1, 3, 'S')
+        S2(2, 0, 0)
+        kk(1, 0, 0)
+        S2(2, 0, 1)
+        S2(2, 1, 0)
+        q2(1, 1)
+        S2(2, 1, 1)
+        S2(2, 2, 0)
+        hh(2, 0)
+        S2(2, 2, 1)
+        S2(2, 3, 0)
+        kk(1, 0, 1)
+        S2(2, 3, 1)
+        S2(2, 4, 0)
+        hh(2, 1)
+        S2(2, 4, 1)
+        S3(1, 0, 3)
+        kk(1, 0, 2)
+        S2(2, 5, 0)
+        S2(2, 5, 1)
+        hh(2, 2)
+        S2(2, 6, 0)
+        S2(2, 6, 1)
+        kk(1, 0, 3)
+        S2(2, 7, 0)
+        S2(2, 7, 1)
+        hh(2, 3)
         S3(1, 1, 0)
-        kk(1, 1, 2, 'V')
+        S3(1, 1, 1)
+        hh(2, 4)
+        T(2, 0)
+        kk(1, 1, 0)
+        S3(1, 1, 2)
+        f(2, 0, 'S')
         S3(1, 1, 3)
-        kkG(1, 1, 1)
-        kkS(1, 1, 3)
-        kk(1, 1, 0, 'V')
-        kkG(1, 1, 3)
+        hh(2, 5)
+        T(2, 1)
+        kk(1, 1, 1)
+        f(2, 1, 'S')
+        hh(2, 6)
+        q2(2, 0)
+        hh(2, 7)
+        S3(2, 0, 0)
+        T(2, 2)
+        kk(1, 1, 2)
+        T(2, 3)
+        kk(1, 1, 3)
+        f(2, 2, 'S')
+        S3(2, 0, 1)
+        S3(2, 0, 2)
+        kk(2, 0, 0)
+        f(2, 3, 'S')
+        S3(2, 0, 3)
+        kk(2, 0, 1)
+        q2(2, 1)
+        kk(2, 0, 2)
+        S3(2, 1, 0)
+        S3(2, 1, 1)
+        kk(2, 0, 3)
+        S3(2, 1, 2)
+        S3(2, 1, 3)
+        kk(2, 1, 0)
+        kk(2, 1, 1)
+        kk(2, 1, 2)
+        kk(2, 1, 3)

@@ -35,21 +35,19 @@ def tile_water_zone_transfer_t2_kernel(
         zone_s = keep.tile([P, 3, 512], U8, name="zone_s", align_bytes=64)
         valve_b = keep.tile([P, 3072], BF16, name="valve_b", align_bytes=64)
         ident = keep.tile([P, P], F32, name="ident", align_bytes=64)
-        ident_b = keep.tile([P, P], BF16, name="ident_b", align_bytes=64)
         warm = keep.tile([P, 2], F32, name="warm", align_bytes=64)
         xr = [[keep.tile([P, 4, 512], BF16, name="xr%d%d" % (g, h), align_bytes=64) for h in range(2)] for g in range(3)]
         xq = [[keep.tile([P, 512], U32, name="xq%d%d" % (g, h), align_bytes=64) for h in range(2)] for g in range(3)]
         xs = [[keep.tile([P, 512], U8, name="xs%d%d" % (g, h), align_bytes=64) for h in range(2)] for g in range(3)]
-        xt = [keep.tile([P, 8, 512], BF16, name="xt%d" % z, align_bytes=64) for z in range(3)]
+        xt = [keep.tile([P, 4, 512, 2], BF16, name="xt%d" % z, align_bytes=64) for z in range(3)]
         h1 = [keep.tile([P, 8, 512], F32, name="h1_%d" % z, align_bytes=64) for z in range(3)]
         xi, h1b, h1q, h1s, h2t, h2i, h2q, h2s, banks, dts, kts = {}, {}, {}, {}, {}, {}, {}, {}, {}, {}, {}
 
         nc.vector.memset(u_s[:].rearrange("p g n -> p (g n)").bitcast(I32), 0)
         nc.gpsimd.memset(warm[:], 0.0)
-        make_identity(nc, ident_b[:])
+        make_identity(nc, ident[:])
         nc.gpsimd.memset(mix_s[:].rearrange("p g n -> p (g n)").bitcast(I32), 0)
         nc.gpsimd.memset(zone_s[:].rearrange("p g n -> p (g n)").bitcast(I32), 0)
-        make_identity(nc, ident[:])
         nc.scalar.copy(out=warm[:, 1:2], in_=warm[:, 0:1])
 
         up_v = up_words.rearrange("g p n -> p g n")
@@ -130,16 +128,16 @@ def tile_water_zone_transfer_t2_kernel(
             banks[key] = t
             return t
 
-        def X(z, m):
-            bk = bank(("x", z, m), BF16)
-            src = xr[z][m // 4][:].rearrange("p j (q t) -> p j t q", t=4)
+        def X(z, gu):
+            bk = bank(("x", z, gu))
             for j in range(4):
-                nc.tensor.transpose(bk[:, j * P : (j + 1) * P], src[:, j, m % 4, :], ident_b[:])
+                words = xr[z][gu // 2][:, j, :].bitcast(F32).rearrange("p (q u) -> p u q", u=2)
+                nc.tensor.transpose(bk[:, j * P : (j + 1) * P], words[:, gu % 2, :], ident[:])
 
-        def y(z, m):
+        def y(z, gu):
             nc.scalar.copy(
-                out=xt[z][:, m, :].rearrange("p (q j) -> p q j", j=4),
-                in_=banks["x", z, m][:].rearrange("p (j q) -> p q j", j=4),
+                out=xt[z][:, gu, :, :].rearrange("p n e -> p (n e)").bitcast(F32).rearrange("p (q j) -> p q j", j=4),
+                in_=banks["x", z, gu][:].rearrange("p (j q) -> p q j", j=4),
             )
 
         def S1p(z, m, g):
@@ -157,7 +155,7 @@ def tile_water_zone_transfer_t2_kernel(
             )
 
         def dd(z, m):
-            nc.vector.tensor_tensor(out=h1[z][:, m, :], in0=banks["1", z, m][:], in1=xt[z][:, m, :], op=ALU.add)
+            nc.vector.tensor_tensor(out=h1[z][:, m, :], in0=banks["1", z, m][:], in1=xt[z][:, m // 2, :, m % 2], op=ALU.add)
 
         def ddS(z, m):
             dt = work.tile([P, 512], F32, name="dt", bufs=3, align_bytes=64)
@@ -165,7 +163,7 @@ def tile_water_zone_transfer_t2_kernel(
             nc.scalar.copy(out=dt[:], in_=banks["1", z, m][:])
 
         def ddG(z, m):
-            nc.gpsimd.tensor_tensor(out=h1[z][:, m, :], in0=dts[z, m][:], in1=xt[z][:, m, :], op=ALU.add)
+            nc.gpsimd.tensor_tensor(out=h1[z][:, m, :], in0=dts[z, m][:], in1=xt[z][:, m // 2, :, m % 2], op=ALU.add)
 
         def e(z, h, n):
             if n == 0:
@@ -248,7 +246,7 @@ def tile_water_zone_transfer_t2_kernel(
             )
 
         def kfin(z, hf, m, eng, src):
-            o = work.tile([P, 512], F32, name="o", bufs=6, align_bytes=64)
+            o = work.tile([P, 512], F32, name="o", bufs=8, align_bytes=64)
             gate = valve_b[:, z * 1024 + hf * 512 : z * 1024 + (hf + 1) * 512]
             eng.tensor_tensor(
                 out=o[:].rearrange("p (q t) -> p q t", t=4),
@@ -280,319 +278,303 @@ def tile_water_zone_transfer_t2_kernel(
         b(0, 0)
         X(1, 0)
         aS(1, 0, 256)
-        X(0, 2)
         aV(1, 0, 256)
         X(1, 1)
-        X(1, 2)
-        y(0, 1)
         b(1, 0)
-        X(1, 3)
-        y(0, 2)
-        X(0, 3)
+        S1p(0, 0, 0)
+        aS(2, 0, 256)
         aV(2, 0, 256)
+        S1p(0, 1, 0)
         X(2, 0)
         y(1, 0)
-        S1p(0, 0, 0)
-        y(0, 3)
-        S1p(0, 1, 0)
-        y(1, 1)
-        S1p(0, 0, 1)
-        aS(2, 0, 256)
-        S1p(0, 2, 0)
-        S1p(0, 1, 1)
-        aV(0, 1, 256)
-        X(2, 1)
-        aS(0, 1, 256)
         b(2, 0)
-        S1p(0, 3, 0)
-        aV(1, 1, 256)
-        S1p(0, 2, 1)
-        y(1, 2)
+        X(2, 1)
+        y(0, 1)
+        S1p(0, 2, 0)
+        aV(0, 1, 256)
+        aS(0, 1, 256)
+        S1p(0, 0, 1)
         S1p(0, 0, 2)
-        S1p(0, 3, 1)
-        aS(1, 1, 256)
-        b(0, 1)
-        S1p(0, 1, 2)
-        S1p(0, 2, 2)
-        dd(0, 0)
-        X(2, 2)
-        dd(0, 1)
-        S1p(0, 3, 2)
+        S1p(0, 3, 0)
         y(2, 0)
-        S1p(0, 4, 0)
-        b(1, 1)
-        y(1, 3)
-        S1p(0, 5, 0)
-        S1p(0, 6, 0)
-        dd(0, 2)
-        aS(2, 1, 256)
-        S1p(0, 4, 1)
-        S1p(0, 7, 0)
+        aV(1, 1, 256)
+        S1p(0, 1, 1)
+        S1p(0, 1, 2)
+        aS(1, 1, 256)
+        S1p(0, 2, 1)
+        b(0, 1)
+        S1p(0, 3, 1)
+        S1p(0, 2, 2)
         aV(2, 1, 256)
+        S1p(0, 3, 2)
+        S1p(0, 4, 0)
+        y(2, 1)
+        X(1, 2)
+        dd(0, 0)
+        y(1, 1)
+        X(0, 2)
+        b(1, 1)
+        y(1, 2)
+        S1p(0, 5, 0)
+        dd(0, 1)
+        S1p(0, 4, 1)
+        aS(2, 1, 256)
+        S1p(0, 6, 0)
+        cM(0, 0)
         S1p(0, 5, 1)
         S1p(0, 6, 1)
-        dd(0, 3)
+        dd(0, 2)
+        S1p(0, 7, 0)
+        y(0, 2)
         S1p(0, 7, 1)
-        y(2, 1)
-        X(0, 4)
+        X(0, 3)
         b(2, 1)
-        y(2, 2)
-        X(2, 3)
-        X(0, 5)
-        cN()
-        y(2, 3)
-        X(1, 4)
+        X(1, 3)
+        dd(0, 3)
         S1p(0, 4, 2)
-        y(0, 4)
-        S1p(0, 5, 2)
-        S1p(0, 6, 2)
-        cM(0, 0)
-        y(0, 5)
-        S1p(0, 7, 2)
-        X(0, 6)
-        dd(0, 4)
-        y(1, 4)
-        X(1, 5)
-        dd(0, 5)
-        y(0, 6)
-        X(2, 4)
-        X(0, 7)
-        y(1, 5)
-        X(2, 5)
-        dd(0, 6)
-        X(1, 6)
-        y(0, 7)
-        X(2, 6)
         cM(0, 1)
-        X(2, 7)
-        y(1, 6)
-        X(1, 7)
-        dd(0, 7)
+        y(1, 3)
+        S1p(0, 5, 2)
+        cN()
         S1p(1, 0, 0)
         e(0, 0, 0)
-        cM(1, 0)
         S1p(1, 0, 1)
         S1p(1, 0, 2)
-        cM(1, 1)
+        S1p(0, 6, 2)
+        dd(0, 4)
         S1p(1, 1, 0)
         S1p(1, 1, 1)
         e(0, 0, 1)
-        dd(1, 0)
         S1p(1, 1, 2)
+        cM(1, 0)
         S1p(1, 2, 0)
-        dd(1, 1)
         S1p(1, 2, 1)
+        dd(0, 5)
         S1p(1, 2, 2)
+        y(0, 3)
         S1p(1, 3, 0)
-        e(0, 1, 0)
-        q1(0, 0)
+        cM(1, 1)
         S1p(1, 3, 1)
         S1p(1, 3, 2)
-        dd(1, 2)
+        dd(0, 6)
+        S1p(0, 7, 2)
         S1p(1, 4, 0)
+        dd(0, 7)
         S1p(1, 4, 1)
-        dd(1, 3)
-        e(0, 1, 1)
         S1p(1, 4, 2)
         S1p(1, 5, 0)
-        dd(1, 4)
+        q1(0, 0)
+        e(0, 1, 0)
         S1p(1, 5, 1)
         S1p(1, 5, 2)
+        dd(1, 0)
         S1p(1, 6, 0)
-        y(1, 7)
-        dd(1, 5)
         S1p(1, 6, 1)
+        dd(1, 1)
         S1p(1, 6, 2)
-        y(2, 4)
-        q1(0, 1)
+        e(0, 1, 1)
         S1p(1, 7, 0)
+        dd(1, 2)
         S1p(1, 7, 1)
-        e(1, 0, 0)
-        dd(1, 6)
         S1p(1, 7, 2)
+        dd(1, 3)
+        X(2, 2)
+        q1(0, 1)
+        e(1, 0, 0)
+        X(2, 3)
+        dd(1, 4)
         S2(0, 0, 0)
-        dd(1, 7)
         S2(0, 0, 1)
+        dd(1, 5)
+        y(2, 2)
         S2(0, 1, 0)
-        e(1, 0, 1)
-        hh(0, 0)
         S2(0, 1, 1)
+        hh(0, 0)
+        e(1, 0, 1)
         S2(0, 2, 0)
-        hh(0, 1)
         S2(0, 2, 1)
-        S2(0, 3, 0)
-        S2(0, 3, 1)
-        hh(0, 2)
-        e(1, 1, 0)
-        S2(0, 4, 0)
-        S2(0, 4, 1)
-        hh(0, 3)
-        T(0, 0)
-        q1(1, 0)
-        e(1, 1, 1)
-        S2(0, 5, 0)
-        S2(0, 5, 1)
-        hh(0, 4)
+        dd(1, 6)
         S1p(2, 0, 0)
         S1p(2, 0, 1)
-        hh(0, 5)
+        hh(0, 1)
         S1p(2, 0, 2)
-        y(2, 5)
-        S2(0, 6, 0)
-        dd(2, 0)
-        f(0, 0, 'S')
-        S2(0, 6, 1)
-        T(0, 1)
-        hh(0, 6)
-        y(2, 6)
+        S2(0, 3, 0)
+        dd(1, 7)
+        S2(0, 3, 1)
+        S2(0, 4, 0)
+        q1(1, 0)
+        S2(0, 4, 1)
+        e(1, 1, 0)
+        T(0, 0)
+        hh(0, 2)
         S1p(2, 1, 0)
-        f(0, 1, 'S')
-        q1(1, 1)
         S1p(2, 1, 1)
+        hh(0, 3)
+        e(1, 1, 1)
         S1p(2, 1, 2)
+        S2(0, 5, 0)
+        hh(0, 4)
+        S2(0, 5, 1)
+        S2(0, 6, 0)
+        hh(0, 5)
+        S2(0, 6, 1)
+        f(0, 0, 'S')
+        T(0, 1)
+        q1(1, 1)
+        S1p(2, 2, 0)
+        f(0, 1, 'S')
+        S1p(2, 2, 1)
+        hh(0, 6)
+        S1p(2, 2, 2)
         S2(0, 7, 0)
         q2(0, 0)
         S2(0, 7, 1)
-        S1p(2, 2, 0)
-        hh(0, 7)
-        S1p(2, 2, 1)
-        S1p(2, 2, 2)
-        dd(2, 1)
-        S3(0, 0, 0)
-        S2(1, 0, 0)
-        kk(0, 0, 0)
-        S2(1, 0, 1)
-        T(0, 2)
-        dd(2, 2)
-        S3(0, 0, 1)
-        f(0, 2, 'S')
-        hh(1, 0)
         S1p(2, 3, 0)
         S1p(2, 3, 1)
-        y(2, 7)
-        kk(0, 0, 1)
+        dd(2, 0)
         S1p(2, 3, 2)
+        S2(1, 0, 0)
+        hh(0, 7)
+        S2(1, 0, 1)
+        T(0, 2)
+        dd(2, 1)
         S2(1, 1, 0)
-        dd(2, 3)
+        dd(2, 2)
+        f(0, 2, 'S')
         S2(1, 1, 1)
-        S3(0, 0, 2)
-        hh(1, 1)
         S1p(2, 4, 0)
+        hh(1, 0)
         S1p(2, 4, 1)
-        kk(0, 0, 2)
         S1p(2, 4, 2)
-        S2(1, 2, 0)
-        dd(2, 4)
-        S2(1, 2, 1)
-        S3(0, 0, 3)
-        hh(1, 2)
+        dd(2, 3)
+        S3(0, 0, 0)
         T(0, 3)
-        T(1, 0)
-        kk(0, 0, 3)
+        kk(0, 0, 0)
+        S3(0, 0, 1)
         f(0, 3, 'S')
-        S2(1, 3, 0)
-        S2(1, 3, 1)
-        f(1, 0, 'S')
-        q2(0, 1)
+        hh(1, 1)
+        S2(1, 2, 0)
+        S2(1, 2, 1)
+        y(2, 3)
         S1p(2, 5, 0)
+        dd(2, 4)
         S1p(2, 5, 1)
-        e(2, 0, 0)
-        hh(1, 3)
+        kkS(0, 0, 1)
         S1p(2, 5, 2)
-        S3(0, 1, 0)
+        hh(1, 2)
+        S3(0, 0, 2)
+        e(2, 0, 0)
+        S2(1, 3, 0)
+        kkG(0, 0, 1)
         dd(2, 5)
+        S2(1, 3, 1)
+        S1p(2, 6, 0)
+        kk(0, 0, 2)
+        S1p(2, 6, 1)
+        S1p(2, 6, 2)
+        e(2, 0, 1)
+        q2(0, 1)
+        S3(0, 0, 3)
         S2(1, 4, 0)
         S2(1, 4, 1)
-        e(2, 0, 1)
-        kk(0, 1, 0)
-        S1p(2, 6, 0)
-        S1p(2, 6, 1)
-        hh(1, 4)
-        S1p(2, 6, 2)
-        S3(0, 1, 1)
         dd(2, 6)
-        S2(1, 5, 0)
-        S2(1, 5, 1)
-        kk(0, 1, 1)
         S1p(2, 7, 0)
+        kkS(0, 0, 3)
         S1p(2, 7, 1)
-        hh(1, 5)
+        hh(1, 3)
         S1p(2, 7, 2)
-        T(1, 1)
+        S3(0, 1, 0)
+        kkG(0, 0, 3)
+        dd(2, 7)
+        T(1, 0)
+        S2(1, 5, 0)
+        hh(1, 4)
+        e(2, 1, 0)
+        S2(1, 5, 1)
+        S3(0, 1, 1)
         q1(2, 0)
         S2(1, 6, 0)
-        f(1, 1, 'S')
-        dd(2, 7)
         S2(1, 6, 1)
+        hh(1, 5)
+        f(1, 0, 'S')
+        T(1, 1)
+        kk(0, 1, 0)
         S3(0, 1, 2)
-        hh(1, 6)
-        S2(1, 7, 0)
-        e(2, 1, 0)
-        S2(1, 7, 1)
-        kk(0, 1, 2)
-        S3(0, 1, 3)
-        T(1, 2)
-        hh(1, 7)
         e(2, 1, 1)
-        q2(1, 0)
-        T(1, 3)
-        kk(0, 1, 3)
-        S3(1, 0, 0)
-        f(1, 2, 'S')
-        S3(1, 0, 1)
+        S2(1, 7, 0)
+        hh(1, 6)
+        S2(1, 7, 1)
+        S3(0, 1, 3)
+        hh(1, 7)
+        T(1, 2)
+        f(1, 1, 'S')
         q1(2, 1)
-        S3(1, 0, 2)
-        f(1, 3, 'S')
+        T(1, 3)
+        f(1, 2, 'S')
         S2(2, 0, 0)
-        kk(1, 0, 0)
+        q2(1, 0)
+        kkS(0, 1, 1)
         S2(2, 0, 1)
+        kk(0, 1, 2)
+        f(1, 3, 'S')
+        S3(1, 0, 0)
+        kkG(0, 1, 1)
         S2(2, 1, 0)
-        q2(1, 1)
+        kk(1, 0, 0)
         S2(2, 1, 1)
+        S3(1, 0, 1)
         S2(2, 2, 0)
-        hh(2, 0)
+        q2(1, 1)
+        kkS(1, 0, 1)
         S2(2, 2, 1)
+        S3(1, 0, 2)
+        hh(2, 0)
         S2(2, 3, 0)
-        kk(1, 0, 1)
+        kkS(0, 1, 3)
         S2(2, 3, 1)
+        kk(1, 0, 2)
+        S3(1, 0, 3)
+        kkG(0, 1, 3)
         S2(2, 4, 0)
         hh(2, 1)
+        kkS(1, 0, 3)
         S2(2, 4, 1)
-        S3(1, 0, 3)
-        kk(1, 0, 2)
         S2(2, 5, 0)
-        S2(2, 5, 1)
         hh(2, 2)
-        S2(2, 6, 0)
-        S2(2, 6, 1)
-        kk(1, 0, 3)
-        S2(2, 7, 0)
-        S2(2, 7, 1)
-        hh(2, 3)
+        S2(2, 5, 1)
+        kkG(1, 0, 1)
         S3(1, 1, 0)
+        hh(2, 3)
+        T(2, 0)
+        S2(2, 6, 0)
+        kk(1, 1, 0)
+        kkG(1, 0, 3)
+        f(2, 0, 'S')
+        S2(2, 6, 1)
         S3(1, 1, 1)
         hh(2, 4)
-        T(2, 0)
-        kk(1, 1, 0)
-        S3(1, 1, 2)
-        f(2, 0, 'S')
-        S3(1, 1, 3)
-        hh(2, 5)
         T(2, 1)
-        kk(1, 1, 1)
+        kkS(1, 1, 1)
+        hh(2, 5)
+        S2(2, 7, 0)
         f(2, 1, 'S')
+        S2(2, 7, 1)
         hh(2, 6)
-        q2(2, 0)
-        hh(2, 7)
-        S3(2, 0, 0)
+        kkG(1, 1, 1)
+        S3(1, 1, 2)
         T(2, 2)
-        kk(1, 1, 2)
+        hh(2, 7)
+        S3(1, 1, 3)
+        q2(2, 0)
         T(2, 3)
-        kk(1, 1, 3)
+        kkS(1, 1, 3)
+        kk(1, 1, 2)
+        S3(2, 0, 0)
         f(2, 2, 'S')
+        kkG(1, 1, 3)
         S3(2, 0, 1)
-        S3(2, 0, 2)
         kk(2, 0, 0)
+        S3(2, 0, 2)
         f(2, 3, 'S')
         S3(2, 0, 3)
         kk(2, 0, 1)

@@ -107,9 +107,10 @@ def tile_water_zone_transfer_t2_kernel(
             if (g, h) not in xi:
                 t = work.tile([P, 4, P, 4], BF16, name="xi", bufs=3, align_bytes=64)
                 xi[g, h] = t
+            rows = slice(t0 * 32, t1 * 32)
             copy(
-                out=xi[g, h][:, t0:t1, :, :],
-                in_=xr[g][h][:].rearrange("p j (q t) -> p t q j", t=4)[:, t0:t1, :, :],
+                out=xi[g, h][:].rearrange("p t q j -> p q t j")[:, rows, :, :],
+                in_=xr[g][h][:].rearrange("p j (q t) -> p q t j", t=4)[:, rows, :, :],
             )
 
         def aV(g, h, fr):

from contextlib import ExitStack

import concourse.mybir as mybir
from concourse.masks import make_identity

ZONES, L, NODES, C = 3, 512, 1536, 1024
FLOPS = 2 * (NODES * NODES * C + NODES * C * C + NODES * L * C)
F32 = mybir.dt.float32
BF16 = mybir.dt.bfloat16
U32 = mybir.dt.uint32
I32 = mybir.dt.int32
U8 = mybir.dt.uint8
FP8X4 = mybir.dt.float8_e4m3fn_x4
FP4X4 = mybir.dt.float4_e2m1fn_x4
P = 128
ALU = mybir.AluOpType

def tile_water_zone_transfer_t2_kernel(
    tc, x, up_words, up_scales, mix_words, mix_scales, zone_words, zone_scales, valve, out
):
    nc = tc.nc
    with ExitStack() as ctx:
        keep = ctx.enter_context(tc.tile_pool(name="keep", bufs=1))
        work = ctx.enter_context(tc.tile_pool(name="work", bufs=3))
        psum = ctx.enter_context(tc.psum_pool(name="psum", bufs=1))
        ctx.enter_context(tc.manual_schedule())

        u_w = [keep.tile([P, 3, 1024], U8, name="u_w%d" % z, align_bytes=64) for z in range(3)]
        u_s = keep.tile([P, 3, 1536], U8, name="u_s", align_bytes=64)
        mix_w = keep.tile([P, 2, 2048], U8, name="mix_w", align_bytes=64)
        mix_s = keep.tile([P, 2, 1024], U8, name="mix_s", align_bytes=64)
        mixp_w = keep.tile([P, 2, 2048], U8, name="mixp_w", align_bytes=64)
        mixp_s = keep.tile([P, 2, 1024], U8, name="mixp_s", align_bytes=64)
        zone_w = keep.tile([P, 3, 1024], U8, name="zone_w", align_bytes=64)
        zone_s = keep.tile([P, 3, 512], U8, name="zone_s", align_bytes=64)
        valve_b = keep.tile([P, 3072], BF16, name="valve_b", align_bytes=64)
        ident = keep.tile([P, P], F32, name="ident", align_bytes=64)
        warm = keep.tile([P, 2], F32, name="warm", align_bytes=64)
        xr = [[keep.tile([P, 4, 512], BF16, name="xr%d%d" % (g, h), align_bytes=64) for h in range(2)] for g in range(3)]
        xq = [[keep.tile([P, 512], U32, name="xq%d%d" % (g, h), align_bytes=64) for h in range(2)] for g in range(3)]
        xs = [[keep.tile([P, 512], U8, name="xs%d%d" % (g, h), align_bytes=64) for h in range(2)] for g in range(3)]
        xt = [keep.tile([P, 4, 512, 2], BF16, name="xt%d" % z, align_bytes=64) for z in range(3)]
        h1 = [keep.tile([P, 8, 512], F32, name="h1_%d" % z, align_bytes=64) for z in range(3)]
        xi, h1b, h1q, h1s, h2t, h2i, h2q, h2s, banks, dts, kts = {}, {}, {}, {}, {}, {}, {}, {}, {}, {}, {}

        nc.vector.memset(u_s[:].rearrange("p g n -> p (g n)").bitcast(I32), 0)
        nc.gpsimd.memset(warm[:], 0.0)
        make_identity(nc, ident[:])
        nc.gpsimd.memset(mix_s[:].rearrange("p g n -> p (g n)").bitcast(I32), 0)
        nc.gpsimd.memset(zone_s[:].rearrange("p g n -> p (g n)").bitcast(I32), 0)
        nc.scalar.copy(out=warm[:, 1:2], in_=warm[:, 0:1])

        up_v = up_words.rearrange("g p n -> p g n")
        x_v = x.rearrange("(g p j) c -> g p j c", p=P, j=4)

        def load_u(z):
            nc.sync.dma_start(out=u_w[z][:].bitcast(I32), in_=up_v[:, :, z * 1024 : (z + 1) * 1024].bitcast(I32))

        def load_scales(tile, src):
            src_v = src.rearrange("g (q r) n -> r q g n", r=4)
            for r in range(4):
                nc.sync.dma_start(out=tile[r:P:32, :, :].bitcast(I32), in_=src_v[r].bitcast(I32))

        def load_x(g, h):
            nc.sync.dma_start(out=xr[g][h][:], in_=x_v[g][:, :, h * 512 : (h + 1) * 512])

        def load_mix():
            nc.sync.dma_start(out=mix_w[:].bitcast(I32), in_=mix_words.rearrange("g p n -> p g n").bitcast(I32))

        def load_zone():
            nc.sync.dma_start(out=zone_w[:].bitcast(I32), in_=zone_words.rearrange("g p n -> p g n").bitcast(I32))

        def load_valve():
            nc.sync.dma_start(out=valve_b[:], in_=valve.rearrange("z c -> (z c)").partition_broadcast(P))


        load_x(0, 0)
        load_x(1, 0)
        load_u(0)
        load_x(2, 0)
        load_scales(u_s, up_scales)
        for g in range(3):
            load_x(g, 1)
        load_u(1)
        load_scales(mix_s, mix_scales)
        load_mix()
        load_u(2)
        load_scales(zone_s, zone_scales)
        load_zone()
        load_valve()


        def cM(g, gc):
            cols = slice(gc * 1024, (gc + 1) * 1024)
            nc.vector.tensor_copy(
                out=mixp_w[:, g, cols].rearrange("p (t q b) -> p t q b", t=4, b=2),
                in_=mix_w[:, g, cols].rearrange("p (q t b) -> p t q b", t=4, b=2),
            )

        def cN():
            nc.vector.tensor_copy(
                out=mixp_s[:].rearrange("p g (h t q) -> p (g h) t q", h=2, t=4),
                in_=mix_s[:].rearrange("p g (h q t) -> p (g h) t q", h=2, t=4),
            )

        def inter(copy, g, h, t0, t1):
            if (g, h) not in xi:
                t = work.tile([P, 4, P, 4], BF16, name="xi", bufs=3, align_bytes=64)
                xi[g, h] = t
            rows = slice(t0 * 32, t1 * 32)
            copy(
                out=xi[g, h][:].rearrange("p t q j -> p q t j")[:, rows, :, :],
                in_=xr[g][h][:].rearrange("p j (q t) -> p q t j", t=4)[:, rows, :, :],
            )

        def aV(g, h, fr):
            inter(nc.vector.tensor_copy, g, h, 0, fr // P)

        def aS(g, h, fr):
            inter(nc.scalar.copy, g, h, fr // P, 4)

        def b(g, h):
            nc.vector.quantize_mx(
                out=xq[g][h][:].bitcast(FP8X4), scales=xs[g][h][:], in_=xi[g, h][:].rearrange("p t q j -> p (t q j)")
            )

        def bank(key, dtype=F32):
            t = psum.tile([P, 512], dtype, name="bank", tag="bank", bufs=8)
            banks[key] = t
            return t

        def X(z, gu):
            bk = bank(("x", z, gu))
            for j in range(4):
                words = xr[z][gu // 2][:, j, :].bitcast(F32).rearrange("p (q u) -> p u q", u=2)
                nc.tensor.transpose(bk[:, j * P : (j + 1) * P], words[:, gu % 2, :], ident[:])

        def y(z, gu):
            nc.scalar.copy(
                out=xt[z][:, gu, :, :].rearrange("p n e -> p (n e)").bitcast(F32).rearrange("p (q j) -> p q j", j=4),
                in_=banks["x", z, gu][:].rearrange("p (j q) -> p q j", j=4),
            )

        def S1p(z, m, g):
            if g == 0:
                bank(("1", z, m))
            cols = slice((m % 4) * P, (m % 4 + 1) * P)
            nc.tensor.matmul_mx(
                out=banks["1", z, m][:],
                lhsT=xq[g][m // 4][:, cols].bitcast(FP8X4),
                lhsT_scale=xs[g][m // 4][:, cols],
                rhs=u_w[z][:, g, :].bitcast(FP4X4),
                rhs_scale=u_s[:, g, z * 512 : (z + 1) * 512],
                start=(g == 0),
                stop=(g == 2),
            )

        def dd(z, m):
            nc.vector.tensor_tensor(out=h1[z][:, m, :], in0=banks["1", z, m][:], in1=xt[z][:, m // 2, :, m % 2], op=ALU.add)

        def ddS(z, m):
            dt = work.tile([P, 512], F32, name="dt", bufs=3, align_bytes=64)
            dts[z, m] = dt
            nc.scalar.copy(out=dt[:], in_=banks["1", z, m][:])

        def ddG(z, m):
            nc.gpsimd.tensor_tensor(out=h1[z][:, m, :], in0=dts[z, m][:], in1=xt[z][:, m // 2, :, m % 2], op=ALU.add)

        def e(z, h, n):
            if n == 0:
                t_ = work.tile([P, 512, 4], BF16, name="h1b", bufs=2, align_bytes=64)
                h1b[z, h] = t_
            rows = slice(n * 256, (n + 1) * 256)
            nc.scalar.copy(
                out=h1b[z, h][:, rows, :].rearrange("p (n i) t -> p n t i", i=4),
                in_=h1[z][:, 4 * h : 4 * h + 4, rows].rearrange("p t (n i) -> p n t i", i=4),
            )

        def q1(z, h):
            tq = work.tile([P, 512], U32, name="h1q", bufs=4, align_bytes=64)
            ts = work.tile([P, 512], U8, name="h1s", bufs=4, align_bytes=64)
            h1q[z, h], h1s[z, h] = tq, ts
            nc.vector.quantize_mx(
                out=tq[:].bitcast(FP8X4), scales=ts[:], in_=h1b[z, h][:].rearrange("p n t -> p (n t)")
            )

        def S2(z, m, g):
            if g == 0:
                bank(("2", z, m))
            nc.tensor.matmul_mx(
                out=banks["2", z, m][:],
                lhsT=mixp_w[:, g, m * 256 : (m + 1) * 256].bitcast(FP4X4),
                lhsT_scale=mixp_s[:, g, m * P : (m + 1) * P],
                rhs=h1q[z, g][:].bitcast(FP8X4),
                rhs_scale=h1s[z, g][:],
                start=(g == 0),
                stop=(g == 1),
            )

        def hh(z, m):
            t_ = work.tile([P, 512], BF16, name="h2t", bufs=6, align_bytes=64)
            h2t[z, m] = t_
            acc = banks["2", z, m][:].rearrange("p (q u e) -> p u q e", u=2, e=2)
            base = h1[z][:, m, :].rearrange("p (q u e) -> p u q e", u=2, e=2)
            dst = t_[:].rearrange("p (u q e) -> p u q e", u=2, e=2)
            for u in range(2):
                nc.vector.scalar_tensor_tensor(
                    out=dst[:, u, :, :], in0=acc[:, u, :, :], scalar=0.0, in1=base[:, u, :, :], op0=ALU.max, op1=ALU.add
                )

        def T(z, mp):
            bk = bank(("t", z, mp))
            for i in range(2):
                words = h2t[z, 2 * mp + i][:].bitcast(F32).rearrange("p (u w) -> p u w", u=2)
                for u in range(2):
                    nc.tensor.transpose(bk[:, (2 * i + u) * P : (2 * i + u + 1) * P], words[:, u, :], ident[:])

        def f(z, mp, eng):
            if mp % 2 == 0:
                t_ = work.tile([P, 512, 4], BF16, name="h2i", bufs=3, align_bytes=64)
                h2i[z, mp // 2] = t_
            dst = h2i[z, mp // 2][:, (mp % 2) * 256 : (mp % 2 + 1) * 256, :].rearrange("p c t -> p (c t)")
            copy = nc.scalar.copy if eng == "S" else nc.vector.tensor_copy
            copy(
                out=dst.bitcast(F32).rearrange("p (i q u) -> p i q u", i=2, u=2),
                in_=banks["t", z, mp][:].rearrange("p (i u q) -> p i q u", i=2, u=2),
            )

        def q2(z, hf):
            tq = work.tile([P, 512], U32, name="h2q", bufs=3, align_bytes=64)
            ts = work.tile([P, 512], U8, name="h2s", bufs=3, align_bytes=64)
            h2q[z, hf], h2s[z, hf] = tq, ts
            nc.vector.quantize_mx(
                out=tq[:].bitcast(FP8X4), scales=ts[:], in_=h2i[z, hf][:].rearrange("p c t -> p (c t)")
            )

        def S3(z, hf, m):
            bk = bank(("3", z, hf, m))
            nc.tensor.matmul_mx(
                out=bk[:],
                lhsT=zone_w[:, z, m * 256 : (m + 1) * 256].bitcast(FP4X4),
                lhsT_scale=zone_s[:, z, m * P : (m + 1) * P],
                rhs=h2q[z, hf][:].bitcast(FP8X4),
                rhs_scale=h2s[z, hf][:],
                start=True,
                stop=True,
            )

        def kfin(z, hf, m, eng, src):
            o = work.tile([P, 512], F32, name="o", bufs=8, align_bytes=64)
            gate = valve_b[:, z * 1024 + hf * 512 : z * 1024 + (hf + 1) * 512]
            eng.tensor_tensor(
                out=o[:].rearrange("p (q t) -> p q t", t=4),
                in0=src,
                in1=gate.rearrange("p (q t) -> p q t", t=4),
                op=ALU.mult,
            )
            nc.sync.dma_start(out=out[z, m * P : (m + 1) * P, hf * 512 : (hf + 1) * 512], in_=o[:])

        def kk(z, hf, m):
            kfin(z, hf, m, nc.vector, banks["3", z, hf, m][:].rearrange("p (t q) -> p q t", t=4))

        def kkS(z, hf, m):
            kt = work.tile([P, 512], F32, name="kt", bufs=4, align_bytes=64)
            kts[z, hf, m] = kt
            nc.scalar.copy(
                out=kt[:].rearrange("p (q t) -> p q t", t=4),
                in_=banks["3", z, hf, m][:].rearrange("p (t q) -> p q t", t=4),
            )

        def kkG(z, hf, m):
            kfin(z, hf, m, nc.gpsimd, kts[z, hf, m][:].rearrange("p (q t) -> p q t", t=4))

        aV(0, 0, 256)
        aS(0, 0, 256)
        X(0, 0)
        X(0, 1)
        y(0, 0)
        b(0, 0)
        X(1, 0)
        aS(1, 0, 256)
        aV(1, 0, 256)
        X(1, 1)
        b(1, 0)
        S1p(0, 0, 0)
        aS(2, 0, 256)
        aV(2, 0, 256)
        S1p(0, 1, 0)
        X(2, 0)
        y(1, 0)
        b(2, 0)
        X(2, 1)
        y(0, 1)
        S1p(0, 2, 0)
        aV(0, 1, 256)
        aS(0, 1, 256)
        S1p(0, 0, 1)
        S1p(0, 0, 2)
        S1p(0, 3, 0)
        y(2, 0)
        aV(1, 1, 256)
        S1p(0, 1, 1)
        S1p(0, 1, 2)
        aS(1, 1, 256)
        S1p(0, 2, 1)
        b(0, 1)
        S1p(0, 3, 1)
        S1p(0, 2, 2)
        aV(2, 1, 256)
        S1p(0, 3, 2)
        S1p(0, 4, 0)
        y(2, 1)
        X(1, 2)
        dd(0, 0)
        y(1, 1)
        X(0, 2)
        b(1, 1)
        y(1, 2)
        S1p(0, 5, 0)
        dd(0, 1)
        S1p(0, 4, 1)
        aS(2, 1, 256)
        S1p(0, 6, 0)
        cM(0, 0)
        S1p(0, 5, 1)
        S1p(0, 6, 1)
        dd(0, 2)
        S1p(0, 7, 0)
        y(0, 2)
        S1p(0, 7, 1)
        X(0, 3)
        b(2, 1)
        X(1, 3)
        dd(0, 3)
        S1p(0, 4, 2)
        cM(0, 1)
        y(1, 3)
        S1p(0, 5, 2)
        cN()
        S1p(1, 0, 0)
        e(0, 0, 0)
        S1p(1, 0, 1)
        S1p(1, 0, 2)
        S1p(0, 6, 2)
        dd(0, 4)
        S1p(1, 1, 0)
        S1p(1, 1, 1)
        e(0, 0, 1)
        S1p(1, 1, 2)
        cM(1, 0)
        S1p(1, 2, 0)
        S1p(1, 2, 1)
        dd(0, 5)
        S1p(1, 2, 2)
        y(0, 3)
        S1p(1, 3, 0)
        cM(1, 1)
        S1p(1, 3, 1)
        S1p(1, 3, 2)
        dd(0, 6)
        S1p(0, 7, 2)
        S1p(1, 4, 0)
        dd(0, 7)
        S1p(1, 4, 1)
        S1p(1, 4, 2)
        S1p(1, 5, 0)
        q1(0, 0)
        e(0, 1, 0)
        S1p(1, 5, 1)
        S1p(1, 5, 2)
        dd(1, 0)
        S1p(1, 6, 0)
        S1p(1, 6, 1)
        dd(1, 1)
        S1p(1, 6, 2)
        e(0, 1, 1)
        S1p(1, 7, 0)
        dd(1, 2)
        S1p(1, 7, 1)
        S1p(1, 7, 2)
        dd(1, 3)
        X(2, 2)
        q1(0, 1)
        e(1, 0, 0)
        X(2, 3)
        dd(1, 4)
        S2(0, 0, 0)
        S2(0, 0, 1)
        dd(1, 5)
        y(2, 2)
        S2(0, 1, 0)
        S2(0, 1, 1)
        hh(0, 0)
        e(1, 0, 1)
        S2(0, 2, 0)
        S2(0, 2, 1)
        dd(1, 6)
        S1p(2, 0, 0)
        S1p(2, 0, 1)
        hh(0, 1)
        S1p(2, 0, 2)
        S2(0, 3, 0)
        dd(1, 7)
        S2(0, 3, 1)
        S2(0, 4, 0)
        q1(1, 0)
        S2(0, 4, 1)
        e(1, 1, 0)
        T(0, 0)
        hh(0, 2)
        S1p(2, 1, 0)
        S1p(2, 1, 1)
        hh(0, 3)
        e(1, 1, 1)
        S1p(2, 1, 2)
        S2(0, 5, 0)
        hh(0, 4)
        S2(0, 5, 1)
        S2(0, 6, 0)
        hh(0, 5)
        S2(0, 6, 1)
        f(0, 0, 'S')
        T(0, 1)
        q1(1, 1)
        S1p(2, 2, 0)
        f(0, 1, 'S')
        S1p(2, 2, 1)
        hh(0, 6)
        S1p(2, 2, 2)
        S2(0, 7, 0)
        q2(0, 0)
        S2(0, 7, 1)
        S1p(2, 3, 0)
        S1p(2, 3, 1)
        dd(2, 0)
        S1p(2, 3, 2)
        S2(1, 0, 0)
        hh(0, 7)
        S2(1, 0, 1)
        T(0, 2)
        dd(2, 1)
        S2(1, 1, 0)
        dd(2, 2)
        f(0, 2, 'S')
        S2(1, 1, 1)
        S1p(2, 4, 0)
        hh(1, 0)
        S1p(2, 4, 1)
        S1p(2, 4, 2)
        dd(2, 3)
        S3(0, 0, 0)
        T(0, 3)
        kk(0, 0, 0)
        S3(0, 0, 1)
        f(0, 3, 'S')
        hh(1, 1)
        S2(1, 2, 0)
        S2(1, 2, 1)
        y(2, 3)
        S1p(2, 5, 0)
        dd(2, 4)
        S1p(2, 5, 1)
        kkS(0, 0, 1)
        S1p(2, 5, 2)
        hh(1, 2)
        S3(0, 0, 2)
        e(2, 0, 0)
        S2(1, 3, 0)
        kkG(0, 0, 1)
        dd(2, 5)
        S2(1, 3, 1)
        S1p(2, 6, 0)
        kk(0, 0, 2)
        S1p(2, 6, 1)
        S1p(2, 6, 2)
        e(2, 0, 1)
        q2(0, 1)
        S3(0, 0, 3)
        S2(1, 4, 0)
        S2(1, 4, 1)
        dd(2, 6)
        S1p(2, 7, 0)
        kkS(0, 0, 3)
        S1p(2, 7, 1)
        hh(1, 3)
        S1p(2, 7, 2)
        S3(0, 1, 0)
        kkG(0, 0, 3)
        dd(2, 7)
        T(1, 0)
        S2(1, 5, 0)
        hh(1, 4)
        e(2, 1, 0)
        S2(1, 5, 1)
        S3(0, 1, 1)
        q1(2, 0)
        S2(1, 6, 0)
        S2(1, 6, 1)
        hh(1, 5)
        f(1, 0, 'S')
        T(1, 1)
        kk(0, 1, 0)
        S3(0, 1, 2)
        e(2, 1, 1)
        S2(1, 7, 0)
        hh(1, 6)
        S2(1, 7, 1)
        S3(0, 1, 3)
        hh(1, 7)
        T(1, 2)
        f(1, 1, 'S')
        q1(2, 1)
        T(1, 3)
        f(1, 2, 'S')
        S2(2, 0, 0)
        q2(1, 0)
        kkS(0, 1, 1)
        S2(2, 0, 1)
        kk(0, 1, 2)
        f(1, 3, 'S')
        S3(1, 0, 0)
        kkG(0, 1, 1)
        S2(2, 1, 0)
        kk(1, 0, 0)
        S2(2, 1, 1)
        S3(1, 0, 1)
        S2(2, 2, 0)
        q2(1, 1)
        kkS(1, 0, 1)
        S2(2, 2, 1)
        S3(1, 0, 2)
        hh(2, 0)
        S2(2, 3, 0)
        kkS(0, 1, 3)
        S2(2, 3, 1)
        kk(1, 0, 2)
        S3(1, 0, 3)
        kkG(0, 1, 3)
        S2(2, 4, 0)
        hh(2, 1)
        kkS(1, 0, 3)
        S2(2, 4, 1)
        S2(2, 5, 0)
        hh(2, 2)
        S2(2, 5, 1)
        kkG(1, 0, 1)
        S3(1, 1, 0)
        hh(2, 3)
        T(2, 0)
        S2(2, 6, 0)
        kk(1, 1, 0)
        kkG(1, 0, 3)
        f(2, 0, 'S')
        S2(2, 6, 1)
        S3(1, 1, 1)
        hh(2, 4)
        T(2, 1)
        kkS(1, 1, 1)
        hh(2, 5)
        S2(2, 7, 0)
        f(2, 1, 'S')
        S2(2, 7, 1)
        hh(2, 6)
        kkG(1, 1, 1)
        S3(1, 1, 2)
        T(2, 2)
        hh(2, 7)
        S3(1, 1, 3)
        q2(2, 0)
        T(2, 3)
        kkS(1, 1, 3)
        kk(1, 1, 2)
        S3(2, 0, 0)
        f(2, 2, 'S')
        kkG(1, 1, 3)
        S3(2, 0, 1)
        kk(2, 0, 0)
        S3(2, 0, 2)
        f(2, 3, 'S')
        S3(2, 0, 3)
        kk(2, 0, 1)
        q2(2, 1)
        kk(2, 0, 2)
        S3(2, 1, 0)
        S3(2, 1, 1)
        kk(2, 0, 3)
        S3(2, 1, 2)
        S3(2, 1, 3)
        kk(2, 1, 0)
        kk(2, 1, 1)
        kk(2, 1, 2)
        kk(2, 1, 3)
